import numpy as np
import ml_dtypes


def mxq(x, axis, fmt="e4m3"):
    dtype, down = {"e4m3": (ml_dtypes.float8_e4m3fn, 7), "e5m2": (ml_dtypes.float8_e5m2, 14)}[fmt]
    v = np.moveaxis(np.asarray(x, np.float32).astype(ml_dtypes.bfloat16).astype(np.float64), axis, -1)
    blocks = v.reshape(v.shape[:-1] + (-1, 32))
    amax = np.abs(blocks).max(-1, keepdims=True)
    byte = np.maximum(np.where(amax > 0, np.frexp(amax)[1] - 1 + 127, 0) - down, 1)
    scale = np.exp2(byte - 127.0)
    codes = (blocks / scale).astype(np.float32).astype(dtype).astype(np.float64)
    return np.moveaxis((codes * scale).reshape(v.shape), -1, axis)


WIDE = False


def mx_kscale(k):
    if not WIDE:
        return np.ones(k)
    levels = np.array([10, -10, 5, -5, 0])
    if k % 512:
        return np.exp2(np.random.permutation(np.resize(levels, k // 32))).repeat(32)
    a = np.empty((k // 512, 16))
    for p in range(k // 512):
        a[p, :8] = np.random.permutation(np.resize(levels, 8))
        for g in range(8):
            far = levels[np.abs(levels - a[p, g]) >= 10]
            a[p, g + 8] = far[np.random.randint(len(far))]
    return np.exp2(a.ravel()).repeat(32)


def f64(x):
    return np.asarray(x).astype(np.float64)


def striped(idx):
    return np.tile(idx.reshape(-1, 16).T, (8, 1)).astype(np.uint16)


def unstriped(offs):
    return offs[:16].T.reshape(-1).astype(np.int64)


E2M1 = np.array([0.0, 0.5, 1.0, 1.5, 2.0, 3.0, 4.0, 6.0, -0.0, -0.5, -1.0, -1.5, -2.0, -3.0, -4.0, -6.0])


def pack_fp4(w):
    k, n = w.shape
    w = f64(np.asarray(w, np.float32).astype(ml_dtypes.bfloat16)).reshape(k // 32, 32, n)
    amax = np.abs(w).max(1)
    mant, ex = np.frexp(amax / 6.0)
    byte = np.clip(np.where(amax > 0, np.where(mant > 0.5, ex, ex - 1) + 127, 1), 1, 254)
    scaled = (w * np.exp2(127.0 - byte)[:, None, :]).reshape(k, n).astype(np.float32)
    c = np.ascontiguousarray(scaled.reshape(k // 512, 128, 4, n).transpose(0, 1, 3, 2)).astype(ml_dtypes.float4_e2m1fn).view(np.uint8) & 0xF
    words = (c[..., 0::2] | (c[..., 1::2] << 4)).reshape(k // 512, 128, 2 * n)
    return np.ascontiguousarray(words), np.ascontiguousarray(byte.astype(np.uint8).reshape(k // 512, 16, n))


def unpack_fp4(words, scales):
    g, _, n = scales.shape
    words = np.ascontiguousarray(words).reshape(g, 128, n, 2)
    nib = np.empty((g, 128, n, 4), np.uint8)
    nib[..., 0::2] = words & 0xF
    nib[..., 1::2] = words >> 4
    vals = E2M1[nib] * np.repeat(np.exp2(scales.astype(np.float64) - 127.0), 8, axis=1)[..., None]
    return vals.transpose(0, 1, 3, 2).reshape(g * 512, n)


def gelu(v):
    return 0.5 * v * (1.0 + np.tanh(np.sqrt(2.0 / np.pi) * (v + 0.044715 * v**3)))


K, T, S, V, H, N = 1024, 1024, 512, 256, 512, 256


def setup_inputs():
    n = np.random.standard_normal
    s = mx_kscale(K)[:, None]
    u = mx_kscale(H)
    packed_xT = pack_fp4(n((K, T)) * s)
    return {
        "x_words": packed_xT[0],
        "x_scales": packed_xT[1],
        "w1": (n((K, H)) / np.sqrt(K) / s * u).astype(np.float32),
        "w2": (n((H, N)) / np.sqrt(2 * H) / u[:, None]).astype(np.float32),
        "w3": (n((H, N)) / np.sqrt(2 * H) / u[:, None]).astype(np.float32),
        "offs": striped(np.random.permutation(T)[:S]),
    }


def reference(x_words, x_scales, w1, w2, w3, offs):
    xq = unpack_fp4(x_words, x_scales)[:, unstriped(offs)]
    h = gelu(mxq(f64(w1), 0, "e4m3").T @ xq)
    low = 0.5 * (h[:, :V] + h[:, V:2 * V])
    high = 0.5 * (h[:, :V] - h[:, V:2 * V])
    return mxq(f64(w2), 0, "e4m3").T @ mxq(low, 0, "e4m3") + mxq(f64(w3), 0, "e4m3").T @ mxq(high, 0, "e4m3")

@@ -1,0 +1,211 @@
+from contextlib import ExitStack
+
+import concourse.mybir as mybir
+
+K, T, S, V, H, N = 1024, 1024, 512, 256, 512, 256
+FLOPS = 2 * K * H * S + 2 * 2 * H * N * V
+
+F32 = mybir.dt.float32
+BF16 = mybir.dt.bfloat16
+I32 = mybir.dt.int32
+U32 = mybir.dt.uint32
+U16 = mybir.dt.uint16
+U8 = mybir.dt.uint8
+FP8X4 = mybir.dt.float8_e4m3fn_x4
+FP4X4 = mybir.dt.float4_e2m1fn_x4
+GELU = mybir.ActivationFunctionType.Gelu_apprx_tanh
+COPY = mybir.ActivationFunctionType.Copy
+ADD = mybir.AluOpType.add
+SUB = mybir.AluOpType.subtract
+MULT = mybir.AluOpType.mult
+
+P = 128
+PACK = 4
+PASSES = K // (P * PACK)
+HALF = V // 2
+
+
+def tile_picked_haar_gelu_p_kernel(tc, x_words, x_scales, w1, w2, w3, offs, out):
+    nc = tc.nc
+    with ExitStack() as ctx:
+        sb = ctx.enter_context(tc.tile_pool(name="sb", bufs=1))
+        ps = ctx.enter_context(tc.psum_pool(name="ps", bufs=1))
+
+        def tile(shape, dtype, name):
+            return sb.tile(shape, dtype, name=name, align_bytes=64)
+
+        offsets = tile([P, S // 16], U16, "offsets")
+        scale_table = tile([P, T], U8, "scale_table")
+        picked_scales = tile([P, S], U8, "picked_scales")
+        moved_scales = tile([P, S], U8, "moved_scales")
+        word_table = [tile([P, T], U16, "word_table%d" % z) for z in range(PASSES)]
+        picked_words = [tile([P, S], U16, "picked_words%d" % z) for z in range(PASSES)]
+        w1_raw = [[tile([P, PACK, H // 2], F32, "w1_raw%d%d" % (z, c)) for c in range(2)] for z in range(PASSES)]
+        w1_bf = [tile([P, PACK, P, PACK], BF16, "w1_bf%d" % z) for z in range(PASSES)]
+        w1_codes = [[tile([P, 2 * P], U32, "w1_codes%d%d" % (z, u)) for u in range(2)] for z in range(PASSES)]
+        w1_scales = [[tile([P, 2 * P], U8, "w1_scales%d%d" % (z, u)) for u in range(2)] for z in range(PASSES)]
+        wo_raw = []
+        wo_bf = [tile([P, N, PACK], BF16, "wo_bf0")]
+        wo_codes = [tile([P, N], U32, "wo_codes%d" % b) for b in range(2)]
+        wo_scales = [tile([P, N], U8, "wo_scales%d" % b) for b in range(2)]
+        hidden = [tile([P, PACK, 2, HALF], F32, "hidden0")]
+        band_bf = [[tile([P, HALF, PACK], BF16, "band_bf%d%d" % (s, b)) for b in range(2)] for s in range(2)]
+        band_codes = [[tile([P, HALF], U32, "band_codes%d%d" % (s, b)) for b in range(2)] for s in range(2)]
+        band_scales = [[tile([P, HALF], U8, "band_scales%d%d" % (s, b)) for b in range(2)] for s in range(2)]
+        result = [tile([P, 2, HALF], F32, "result%d" % s) for s in range(2)]
+        warm_in = tile([P, 8], F32, "warm_in")
+        warm_out = tile([P, 8], F32, "warm_out")
+        pre = [ps.tile([P, S], F32, name="pre%d" % t) for t in range(PACK)]
+        acc = [[ps.tile([P, HALF], F32, name="acc%d%d" % (s, mb)) for mb in range(2)] for s in range(2)]
+
+        def load_w1(z, c):
+            rows = w1[z * P * PACK : (z + 1) * P * PACK, c * (H // 2) : (c + 1) * (H // 2)]
+            nc.sync.dma_start(out=w1_raw[z][c][:], in_=rows.rearrange("(p j) n -> p j n", j=PACK))
+
+        def load_words(z):
+            nc.sync.dma_start(out=word_table[z][:].bitcast(I32), in_=x_words[z].bitcast(I32))
+
+        def load_wo(b, w):
+            wo_raw.append(sb.tile([P, PACK, N], F32, name="wo_raw%d" % b, tag="w1_raw0%d" % b, align_bytes=64))
+            nc.sync.dma_start(out=wo_raw[b][:], in_=w.rearrange("(p j) n -> p j n", j=PACK))
+
+        def cast_w1(engine_copy, z, c, m0, m1):
+            dst = w1_bf[z][:, :, c * 64 + m0 : c * 64 + m1, :].rearrange("p t m j -> p m j t")
+            src = w1_raw[z][c][:, :, PACK * m0 : PACK * m1].rearrange("p j (m t) -> p m j t", t=PACK)
+            engine_copy(dst, src)
+
+        def quant_w1(z, u):
+            nc.vector.quantize_mx(
+                out=w1_codes[z][u][:].bitcast(FP8X4),
+                scales=w1_scales[z][u][:],
+                in_=w1_bf[z][:, 2 * u : 2 * u + 2, :, :].rearrange("p t m j -> p (t m j)"),
+            )
+
+        def cast_wo(engine_copy, b):
+            dst = wo_bf[b][:].rearrange("p (c i) j -> p c j i", i=2)
+            src = wo_raw[b][:].rearrange("p j (c i) -> p c j i", i=2)
+            engine_copy(dst, src)
+
+        def quant_wo(b):
+            nc.vector.quantize_mx(
+                out=wo_codes[b][:].bitcast(FP8X4), scales=wo_scales[b][:], in_=wo_bf[b][:].rearrange("p n j -> p (n j)")
+            )
+
+        def first_product(z, t):
+            cols = slice((t % 2) * P, (t % 2 + 1) * P)
+            nc.tensor.matmul_mx(
+                out=pre[t][:],
+                lhsT=w1_codes[z][t // 2][:, cols].bitcast(FP8X4),
+                lhsT_scale=w1_scales[z][t // 2][:, cols],
+                rhs=picked_words[z][:].bitcast(FP4X4),
+                rhs_scale=(picked_scales if z == 0 else moved_scales)[:],
+                start=(z == 0),
+                stop=(z == PASSES - 1),
+            )
+
+        def gelu(s, t):
+            src = pre[t][:].rearrange("p (d v) -> p d v", d=2)[:, :, s * HALF : (s + 1) * HALF]
+            nc.scalar.activation(out=hidden[s][:, t, :, :], in_=src, func=GELU)
+
+        def band(s, b):
+            nc.vector.tensor_tensor(
+                out=band_bf[s][b][:].rearrange("p (c i) t -> p c t i", i=2),
+                in0=hidden[s][:, :, 0, :].rearrange("p t (c i) -> p c t i", i=2),
+                in1=hidden[s][:, :, 1, :].rearrange("p t (c i) -> p c t i", i=2),
+                op=(ADD if b == 0 else SUB),
+            )
+
+        def quant_band(s, b):
+            nc.vector.quantize_mx(
+                out=band_codes[s][b][:].bitcast(FP8X4),
+                scales=band_scales[s][b][:],
+                in_=band_bf[s][b][:].rearrange("p v t -> p (v t)"),
+            )
+
+        def second_product(s, b):
+            for mb in range(2):
+                cols = slice(mb * P, (mb + 1) * P)
+                nc.tensor.matmul_mx(
+                    out=acc[s][mb][:],
+                    lhsT=wo_codes[b][:, cols].bitcast(FP8X4),
+                    lhsT_scale=wo_scales[b][:, cols],
+                    rhs=band_codes[s][b][:].bitcast(FP8X4),
+                    rhs_scale=band_scales[s][b][:],
+                    start=(b == 0),
+                    stop=(b == 1),
+                )
+
+        def halve_on_scalar(s, mb):
+            nc.scalar.activation(out=result[s][:, mb, :], in_=acc[s][mb][:], func=COPY, scale=0.5)
+
+        def halve_on_vector(s, mb):
+            nc.vector.tensor_scalar(out=result[s][:, mb, :], in0=acc[s][mb][:], scalar1=0.5, scalar2=None, op0=MULT)
+
+        def store(s):
+            dst = out.rearrange("(mb p) v -> p mb v", p=P)[:, :, s * HALF : (s + 1) * HALF]
+            nc.sync.dma_start(out=dst, in_=result[s][:])
+
+        nc.gpsimd.memset(scale_table[:].bitcast(I32), 0)
+        nc.vector.memset(warm_in[:], 0.0)
+        nc.vector.memset(moved_scales[:].bitcast(I32), 0)
+        nc.sync.dma_start(out=offsets[:], in_=offs)
+        load_words(0)
+        for q in range(4):
+            nc.sync.dma_start(
+                out=scale_table[32 * q : 32 * q + 8, :].bitcast(I32),
+                in_=x_scales[:, 4 * q : 4 * q + 4, :].bitcast(I32),
+            )
+        nc.scalar.activation(out=warm_out[:], in_=warm_in[:], func=GELU)
+        load_w1(0, 0)
+        load_w1(0, 1)
+        load_w1(1, 0)
+        load_words(1)
+        load_w1(1, 1)
+
+        nc.vector.tensor_copy(picked_words[0][:], word_table[0][:].indirect(offsets[:]))
+        nc.vector.tensor_copy(picked_scales[:], scale_table[:].indirect(offsets[:]))
+        nc.sync.dma_start(out=moved_scales[0:100, :].bitcast(I32), in_=picked_scales[4:104, :].bitcast(I32))
+        cast_w1(nc.scalar.copy, 0, 0, 0, 64)
+        load_wo(0, w2)
+        cast_w1(nc.vector.tensor_copy, 0, 1, 0, 44)
+        cast_w1(nc.scalar.copy, 0, 1, 44, 64)
+        load_wo(1, w3)
+        quant_w1(0, 0)
+        quant_w1(0, 1)
+        nc.vector.tensor_copy(picked_words[1][:], word_table[1][:].indirect(offsets[:]))
+        for t in range(PACK):
+            first_product(0, t)
+        cast_w1(nc.scalar.copy, 1, 0, 0, 64)
+        cast_w1(nc.vector.tensor_copy, 1, 1, 0, 42)
+        cast_w1(nc.scalar.copy, 1, 1, 42, 64)
+        quant_w1(1, 0)
+        quant_w1(1, 1)
+        for t in range(PACK):
+            first_product(1, t)
+        hidden.append(sb.tile([P, PACK, 2, HALF], F32, name="hidden1", tag="w1_scales11", align_bytes=64))
+        for s in range(2):
+            for t in range(PACK):
+                gelu(s, t)
+        cast_wo(nc.vector.tensor_copy, 0)
+        wo_bf.append(sb.tile([P, N, PACK], BF16, name="w3_bf", tag="w1_codes11", align_bytes=64))
+        cast_wo(nc.scalar.copy, 1)
+        quant_wo(0)
+        band(0, 0)
+        band(0, 1)
+        quant_band(0, 0)
+        band(1, 0)
+        quant_band(0, 1)
+        band(1, 1)
+        quant_band(1, 0)
+        quant_wo(1)
+        quant_band(1, 1)
+        second_product(0, 0)
+        second_product(1, 0)
+        second_product(0, 1)
+        second_product(1, 1)
+        halve_on_scalar(0, 0)
+        halve_on_scalar(0, 1)
+        store(0)
+        halve_on_scalar(1, 0)
+        halve_on_vector(1, 1)
+        store(1)

@@ -49,7 +49,7 @@ def tile_picked_haar_gelu_p_kernel(tc, x_words, x_scales, w1, w2, w3, offs, out)
         wo_codes = [tile([P, N], U32, "wo_codes%d" % b) for b in range(2)]
         wo_scales = [tile([P, N], U8, "wo_scales%d" % b) for b in range(2)]
         hidden = [tile([P, PACK, 2, HALF], F32, "hidden0")]
-        band_bf = [[tile([P, HALF, PACK], BF16, "band_bf%d%d" % (s, b)) for b in range(2)] for s in range(2)]
+        band_bf = {(s, b): tile([P, HALF, PACK], BF16, "band_bf%d%d" % (s, b)) for s in range(2) for b in range(2) if s or b}
         band_codes = [[tile([P, HALF], U32, "band_codes%d%d" % (s, b)) for b in range(2)] for s in range(2)]
         band_scales = [[tile([P, HALF], U8, "band_scales%d%d" % (s, b)) for b in range(2)] for s in range(2)]
         result = [tile([P, 2, HALF], F32, "result%d" % s) for s in range(2)]
@@ -69,16 +69,17 @@ def tile_picked_haar_gelu_p_kernel(tc, x_words, x_scales, w1, w2, w3, offs, out)
             wo_raw.append(sb.tile([P, PACK, N], F32, name="wo_raw%d" % b, tag="w1_raw0%d" % b, align_bytes=64))
             nc.sync.dma_start(out=wo_raw[b][:], in_=w.rearrange("(p j) n -> p j n", j=PACK))
 
-        def cast_w1(engine_copy, z, c, m0, m1):
-            dst = w1_bf[z][:, :, c * 64 + m0 : c * 64 + m1, :].rearrange("p t m j -> p m j t")
+        def cast_w1(engine_copy, z, c, u, m0, m1):
+            dst = w1_bf[z][:, 2 * u : 2 * u + 2, c * 64 + m0 : c * 64 + m1, :].rearrange("p t m j -> p m j t")
             src = w1_raw[z][c][:, :, PACK * m0 : PACK * m1].rearrange("p j (m t) -> p m j t", t=PACK)
-            engine_copy(dst, src)
+            engine_copy(dst, src[:, :, :, 2 * u : 2 * u + 2])
 
-        def quant_w1(z, u):
+        def quant_w1(z, t0, t1):
+            cols = slice((t0 % 2) * P, (t0 % 2 + t1 - t0) * P)
             nc.vector.quantize_mx(
-                out=w1_codes[z][u][:].bitcast(FP8X4),
-                scales=w1_scales[z][u][:],
-                in_=w1_bf[z][:, 2 * u : 2 * u + 2, :, :].rearrange("p t m j -> p (t m j)"),
+                out=w1_codes[z][t0 // 2][:, cols].bitcast(FP8X4),
+                scales=w1_scales[z][t0 // 2][:, cols],
+                in_=w1_bf[z][:, t0:t1, :, :].rearrange("p t m j -> p (t m j)"),
             )
 
         def cast_wo(engine_copy, b):
@@ -109,7 +110,7 @@ def tile_picked_haar_gelu_p_kernel(tc, x_words, x_scales, w1, w2, w3, offs, out)
 
         def band(s, b):
             nc.vector.tensor_tensor(
-                out=band_bf[s][b][:].rearrange("p (c i) t -> p c t i", i=2),
+                out=band_bf[s, b][:].rearrange("p (c i) t -> p c t i", i=2),
                 in0=hidden[s][:, :, 0, :].rearrange("p t (c i) -> p c t i", i=2),
                 in1=hidden[s][:, :, 1, :].rearrange("p t (c i) -> p c t i", i=2),
                 op=(ADD if b == 0 else SUB),
@@ -119,7 +120,7 @@ def tile_picked_haar_gelu_p_kernel(tc, x_words, x_scales, w1, w2, w3, offs, out)
             nc.vector.quantize_mx(
                 out=band_codes[s][b][:].bitcast(FP8X4),
                 scales=band_scales[s][b][:],
-                in_=band_bf[s][b][:].rearrange("p v t -> p (v t)"),
+                in_=band_bf[s, b][:].rearrange("p v t -> p (v t)"),
             )
 
         def second_product(s, b):
@@ -145,16 +146,17 @@ def tile_picked_haar_gelu_p_kernel(tc, x_words, x_scales, w1, w2, w3, offs, out)
             dst = out.rearrange("(mb p) v -> p mb v", p=P)[:, :, s * HALF : (s + 1) * HALF]
             nc.sync.dma_start(out=dst, in_=result[s][:])
 
+        def store_block(queue, s, mb):
+            queue.dma_start(out=out[mb * P : (mb + 1) * P, s * HALF : (s + 1) * HALF], in_=result[s][:, mb, :])
+
         nc.gpsimd.memset(scale_table[:].bitcast(I32), 0)
         nc.vector.memset(warm_in[:], 0.0)
         nc.vector.memset(moved_scales[:].bitcast(I32), 0)
         nc.sync.dma_start(out=offsets[:], in_=offs)
         load_words(0)
-        for q in range(4):
-            nc.sync.dma_start(
-                out=scale_table[32 * q : 32 * q + 8, :].bitcast(I32),
-                in_=x_scales[:, 4 * q : 4 * q + 4, :].bitcast(I32),
-            )
+        scale_rows = x_scales.rearrange("z (q r) n -> r q z n", r=4)
+        for r in range(4):
+            nc.sync.dma_start(out=scale_table[r:P:16, :].bitcast(I32), in_=scale_rows[r].bitcast(I32))
         nc.scalar.activation(out=warm_out[:], in_=warm_in[:], func=GELU)
         load_w1(0, 0)
         load_w1(0, 1)
@@ -164,22 +166,27 @@ def tile_picked_haar_gelu_p_kernel(tc, x_words, x_scales, w1, w2, w3, offs, out)
 
         nc.vector.tensor_copy(picked_words[0][:], word_table[0][:].indirect(offsets[:]))
         nc.vector.tensor_copy(picked_scales[:], scale_table[:].indirect(offsets[:]))
-        nc.sync.dma_start(out=moved_scales[0:100, :].bitcast(I32), in_=picked_scales[4:104, :].bitcast(I32))
-        cast_w1(nc.scalar.copy, 0, 0, 0, 64)
+        nc.sync.dma_start(out=moved_scales[0:112, :].bitcast(I32), in_=picked_scales[16:128, :].bitcast(I32))
+        cast_w1(nc.scalar.copy, 0, 0, 0, 0, 64)
+        cast_w1(nc.scalar.copy, 0, 0, 1, 0, 64)
         load_wo(0, w2)
-        cast_w1(nc.vector.tensor_copy, 0, 1, 0, 44)
-        cast_w1(nc.scalar.copy, 0, 1, 44, 64)
+        cast_w1(nc.vector.tensor_copy, 0, 1, 0, 0, 64)
+        cast_w1(nc.scalar.copy, 0, 1, 1, 0, 44)
+        cast_w1(nc.vector.tensor_copy, 0, 1, 1, 44, 64)
         load_wo(1, w3)
-        quant_w1(0, 0)
-        quant_w1(0, 1)
+        quant_w1(0, 0, 2)
+        quant_w1(0, 2, 4)
         nc.vector.tensor_copy(picked_words[1][:], word_table[1][:].indirect(offsets[:]))
         for t in range(PACK):
             first_product(0, t)
-        cast_w1(nc.scalar.copy, 1, 0, 0, 64)
-        cast_w1(nc.vector.tensor_copy, 1, 1, 0, 42)
-        cast_w1(nc.scalar.copy, 1, 1, 42, 64)
-        quant_w1(1, 0)
-        quant_w1(1, 1)
+        cast_w1(nc.scalar.copy, 1, 0, 0, 0, 64)
+        cast_w1(nc.scalar.copy, 1, 0, 1, 0, 64)
+        cast_w1(nc.vector.tensor_copy, 1, 1, 0, 0, 64)
+        cast_w1(nc.scalar.copy, 1, 1, 1, 0, 48)
+        cast_w1(nc.vector.tensor_copy, 1, 1, 1, 48, 64)
+        quant_w1(1, 0, 1)
+        quant_w1(1, 1, 2)
+        quant_w1(1, 2, 4)
         for t in range(PACK):
             first_product(1, t)
         hidden.append(sb.tile([P, PACK, 2, HALF], F32, name="hidden1", tag="w1_scales11", align_bytes=64))
@@ -190,6 +197,7 @@ def tile_picked_haar_gelu_p_kernel(tc, x_words, x_scales, w1, w2, w3, offs, out)
         wo_bf.append(sb.tile([P, N, PACK], BF16, name="w3_bf", tag="w1_codes11", align_bytes=64))
         cast_wo(nc.scalar.copy, 1)
         quant_wo(0)
+        band_bf.setdefault((0, 0), sb.tile([P, HALF, PACK], BF16, name="band_bf00", tag="wo_bf0", align_bytes=64))
         band(0, 0)
         band(0, 1)
         quant_band(0, 0)
@@ -208,4 +216,5 @@ def tile_picked_haar_gelu_p_kernel(tc, x_words, x_scales, w1, w2, w3, offs, out)
         store(0)
         halve_on_scalar(1, 0)
         halve_on_vector(1, 1)
-        store(1)
+        store_block(nc.scalar, 1, 0)
+        store_block(nc.sync, 1, 1)

@@ -49,7 +49,7 @@ def tile_picked_haar_gelu_p_kernel(tc, x_words, x_scales, w1, w2, w3, offs, out)
         wo_codes = [tile([P, N], U32, "wo_codes%d" % b) for b in range(2)]
         wo_scales = [tile([P, N], U8, "wo_scales%d" % b) for b in range(2)]
         hidden = [tile([P, PACK, 2, HALF], F32, "hidden0")]
-        band_bf = {(s, b): tile([P, HALF, PACK], BF16, "band_bf%d%d" % (s, b)) for s in range(2) for b in range(2) if s or b}
+        band_bf = []
         band_codes = [[tile([P, HALF], U32, "band_codes%d%d" % (s, b)) for b in range(2)] for s in range(2)]
         band_scales = [[tile([P, HALF], U8, "band_scales%d%d" % (s, b)) for b in range(2)] for s in range(2)]
         result = [tile([P, 2, HALF], F32, "result%d" % s) for s in range(2)]
@@ -69,10 +69,10 @@ def tile_picked_haar_gelu_p_kernel(tc, x_words, x_scales, w1, w2, w3, offs, out)
             wo_raw.append(sb.tile([P, PACK, N], F32, name="wo_raw%d" % b, tag="w1_raw0%d" % b, align_bytes=64))
             nc.sync.dma_start(out=wo_raw[b][:], in_=w.rearrange("(p j) n -> p j n", j=PACK))
 
-        def cast_w1(engine_copy, z, c, u, m0, m1):
-            dst = w1_bf[z][:, 2 * u : 2 * u + 2, c * 64 + m0 : c * 64 + m1, :].rearrange("p t m j -> p m j t")
+        def cast_w1(engine_copy, z, c, t0, t1, m0, m1):
+            dst = w1_bf[z][:, t0:t1, c * 64 + m0 : c * 64 + m1, :].rearrange("p t m j -> p m j t")
             src = w1_raw[z][c][:, :, PACK * m0 : PACK * m1].rearrange("p j (m t) -> p m j t", t=PACK)
-            engine_copy(dst, src[:, :, :, 2 * u : 2 * u + 2])
+            engine_copy(dst, src[:, :, :, t0:t1])
 
         def quant_w1(z, t0, t1):
             cols = slice((t0 % 2) * P, (t0 % 2 + t1 - t0) * P)
@@ -110,7 +110,7 @@ def tile_picked_haar_gelu_p_kernel(tc, x_words, x_scales, w1, w2, w3, offs, out)
 
         def band(s, b):
             nc.vector.tensor_tensor(
-                out=band_bf[s, b][:].rearrange("p (c i) t -> p c t i", i=2),
+                out=band_bf[s][:, b, :, :].rearrange("p (c i) t -> p c t i", i=2),
                 in0=hidden[s][:, :, 0, :].rearrange("p t (c i) -> p c t i", i=2),
                 in1=hidden[s][:, :, 1, :].rearrange("p t (c i) -> p c t i", i=2),
                 op=(ADD if b == 0 else SUB),
@@ -120,7 +120,7 @@ def tile_picked_haar_gelu_p_kernel(tc, x_words, x_scales, w1, w2, w3, offs, out)
             nc.vector.quantize_mx(
                 out=band_codes[s][b][:].bitcast(FP8X4),
                 scales=band_scales[s][b][:],
-                in_=band_bf[s, b][:].rearrange("p v t -> p (v t)"),
+                in_=band_bf[s][:, b, :, :].rearrange("p v t -> p (v t)"),
             )
 
         def second_product(s, b):
@@ -166,24 +166,22 @@ def tile_picked_haar_gelu_p_kernel(tc, x_words, x_scales, w1, w2, w3, offs, out)
 
         nc.vector.tensor_copy(picked_words[0][:], word_table[0][:].indirect(offsets[:]))
         nc.vector.tensor_copy(picked_scales[:], scale_table[:].indirect(offsets[:]))
-        nc.sync.dma_start(out=moved_scales[0:112, :].bitcast(I32), in_=picked_scales[16:128, :].bitcast(I32))
-        cast_w1(nc.scalar.copy, 0, 0, 0, 0, 64)
-        cast_w1(nc.scalar.copy, 0, 0, 1, 0, 64)
+        for p0, p1 in ((0, 64), (64, 96), (96, 112)):
+            nc.sync.dma_start(out=moved_scales[p0:p1, :].bitcast(I32), in_=picked_scales[p0 + 16 : p1 + 16, :].bitcast(I32))
+        cast_w1(nc.scalar.copy, 0, 0, 0, 4, 0, 64)
         load_wo(0, w2)
-        cast_w1(nc.vector.tensor_copy, 0, 1, 0, 0, 64)
-        cast_w1(nc.scalar.copy, 0, 1, 1, 0, 44)
-        cast_w1(nc.vector.tensor_copy, 0, 1, 1, 44, 64)
+        cast_w1(nc.vector.tensor_copy, 0, 1, 0, 4, 0, 44)
+        cast_w1(nc.scalar.copy, 0, 1, 0, 4, 44, 64)
         load_wo(1, w3)
         quant_w1(0, 0, 2)
         quant_w1(0, 2, 4)
         nc.vector.tensor_copy(picked_words[1][:], word_table[1][:].indirect(offsets[:]))
         for t in range(PACK):
             first_product(0, t)
-        cast_w1(nc.scalar.copy, 1, 0, 0, 0, 64)
-        cast_w1(nc.scalar.copy, 1, 0, 1, 0, 64)
-        cast_w1(nc.vector.tensor_copy, 1, 1, 0, 0, 64)
-        cast_w1(nc.scalar.copy, 1, 1, 1, 0, 48)
-        cast_w1(nc.vector.tensor_copy, 1, 1, 1, 48, 64)
+        cast_w1(nc.scalar.copy, 1, 0, 0, 4, 0, 64)
+        cast_w1(nc.vector.tensor_copy, 1, 1, 0, 2, 0, 64)
+        cast_w1(nc.scalar.copy, 1, 1, 2, 4, 0, 44)
+        cast_w1(nc.vector.tensor_copy, 1, 1, 2, 4, 44, 64)
         quant_w1(1, 0, 1)
         quant_w1(1, 1, 2)
         quant_w1(1, 2, 4)
@@ -197,12 +195,13 @@ def tile_picked_haar_gelu_p_kernel(tc, x_words, x_scales, w1, w2, w3, offs, out)
         wo_bf.append(sb.tile([P, N, PACK], BF16, name="w3_bf", tag="w1_codes11", align_bytes=64))
         cast_wo(nc.scalar.copy, 1)
         quant_wo(0)
-        band_bf.setdefault((0, 0), sb.tile([P, HALF, PACK], BF16, name="band_bf00", tag="wo_bf0", align_bytes=64))
+        band_bf.append(sb.tile([P, 2, HALF, PACK], BF16, name="band_bf0", tag="wo_bf0", align_bytes=64))
+        band_bf.append(tile([P, 2, HALF, PACK], BF16, "band_bf1"))
         band(0, 0)
         band(0, 1)
         quant_band(0, 0)
-        band(1, 0)
         quant_band(0, 1)
+        band(1, 0)
         band(1, 1)
         quant_band(1, 0)
         quant_wo(1)
@@ -216,5 +215,4 @@ def tile_picked_haar_gelu_p_kernel(tc, x_words, x_scales, w1, w2, w3, offs, out)
         store(0)
         halve_on_scalar(1, 0)
         halve_on_vector(1, 1)
-        store_block(nc.scalar, 1, 0)
-        store_block(nc.sync, 1, 1)
+        store(1)

@@ -36,55 +36,60 @@ def tile_picked_haar_gelu_p_kernel(tc, x_words, x_scales, w1, w2, w3, offs, out)
 
         offsets = tile([P, S // 16], U16, "offsets")
         scale_table = tile([P, T], U8, "scale_table")
-        picked_scales = tile([P, S], U8, "picked_scales")
-        moved_scales = tile([P, S], U8, "moved_scales")
+        picked_scales = [tile([P, S], U8, "picked_scales"), tile([P, S], U8, "moved_scales")]
         word_table = [tile([P, T], U16, "word_table%d" % z) for z in range(PASSES)]
-        picked_words = [tile([P, S], U16, "picked_words%d" % z) for z in range(PASSES)]
-        w1_raw = [[tile([P, PACK, H // 2], F32, "w1_raw%d%d" % (z, c)) for c in range(2)] for z in range(PASSES)]
-        w1_bf = [tile([P, PACK, P, PACK], BF16, "w1_bf%d" % z) for z in range(PASSES)]
+        picked_words = [tile([P, S], U16, "picked_words0")]
+        w1_raw = [tile([P, PACK, H], F32, "w1_raw%d" % z) for z in range(PASSES)]
+        w1_bf = [[tile([P, 2, P, PACK], BF16, "w1_bf%d%d" % (z, u)) for u in range(2)] for z in range(PASSES)]
         w1_codes = [[tile([P, 2 * P], U32, "w1_codes%d%d" % (z, u)) for u in range(2)] for z in range(PASSES)]
         w1_scales = [[tile([P, 2 * P], U8, "w1_scales%d%d" % (z, u)) for u in range(2)] for z in range(PASSES)]
         wo_raw = []
         wo_bf = [tile([P, N, PACK], BF16, "wo_bf0")]
         wo_codes = [tile([P, N], U32, "wo_codes%d" % b) for b in range(2)]
         wo_scales = [tile([P, N], U8, "wo_scales%d" % b) for b in range(2)]
-        hidden = [tile([P, PACK, 2, HALF], F32, "hidden0")]
+        hidden = [[tile([P, HALF, PACK], F32, "hidden%d%d" % (s, d)) for d in range(2)] for s in range(2)]
         band_bf = []
         band_codes = [[tile([P, HALF], U32, "band_codes%d%d" % (s, b)) for b in range(2)] for s in range(2)]
         band_scales = [[tile([P, HALF], U8, "band_scales%d%d" % (s, b)) for b in range(2)] for s in range(2)]
         result = [tile([P, 2, HALF], F32, "result%d" % s) for s in range(2)]
         warm_in = tile([P, 8], F32, "warm_in")
         warm_out = tile([P, 8], F32, "warm_out")
-        pre = [ps.tile([P, S], F32, name="pre%d" % t) for t in range(PACK)]
+        pre = [[ps.tile([P, PACK, HALF], F32, name="pre%d%d" % (s, d)) for d in range(2)] for s in range(2)]
         acc = [[ps.tile([P, HALF], F32, name="acc%d%d" % (s, mb)) for mb in range(2)] for s in range(2)]
 
-        def load_w1(z, c):
-            rows = w1[z * P * PACK : (z + 1) * P * PACK, c * (H // 2) : (c + 1) * (H // 2)]
-            nc.sync.dma_start(out=w1_raw[z][c][:], in_=rows.rearrange("(p j) n -> p j n", j=PACK))
+        def load_w1(z):
+            rows = w1[z * P * PACK : (z + 1) * P * PACK, :]
+            nc.sync.dma_start(out=w1_raw[z][:], in_=rows.rearrange("(p j) n -> p j n", j=PACK))
 
         def load_words(z):
             nc.sync.dma_start(out=word_table[z][:].bitcast(I32), in_=x_words[z].bitcast(I32))
 
         def load_wo(b, w):
-            wo_raw.append(sb.tile([P, PACK, N], F32, name="wo_raw%d" % b, tag="w1_raw0%d" % b, align_bytes=64))
+            wo_raw.append(sb.tile([P, PACK, N], F32, name="wo_raw%d" % b, tag=("scale_table", "w1_raw0")[b], align_bytes=64))
             nc.sync.dma_start(out=wo_raw[b][:], in_=w.rearrange("(p j) n -> p j n", j=PACK))
 
-        def cast_w1(engine_copy, z, c, t0, t1, m0, m1):
-            dst = w1_bf[z][:, t0:t1, c * 64 + m0 : c * 64 + m1, :].rearrange("p t m j -> p m j t")
-            src = w1_raw[z][c][:, :, PACK * m0 : PACK * m1].rearrange("p j (m t) -> p m j t", t=PACK)
-            engine_copy(dst, src[:, :, :, t0:t1])
+        def cast_w1(engine_copy, z, u, m0, m1):
+            dst = w1_bf[z][u][:, :, m0:m1, :].rearrange("p t m j -> p m j t")
+            src = w1_raw[z][:, :, PACK * m0 : PACK * m1].rearrange("p j (m t) -> p m j t", t=PACK)
+            engine_copy(dst, src[:, :, :, 2 * u : 2 * u + 2])
 
-        def quant_w1(z, t0, t1):
-            cols = slice((t0 % 2) * P, (t0 % 2 + t1 - t0) * P)
+        def round_w1(z):
+            cast_w1(nc.vector.tensor_copy, z, 0, 0, P)
+            cast_w1(nc.scalar.copy, z, 1, 32, P)
+            cast_w1(nc.vector.tensor_copy, z, 1, 0, 32)
+            quant_w1(z, 0)
+            quant_w1(z, 1)
+
+        def quant_w1(z, u):
             nc.vector.quantize_mx(
-                out=w1_codes[z][t0 // 2][:, cols].bitcast(FP8X4),
-                scales=w1_scales[z][t0 // 2][:, cols],
-                in_=w1_bf[z][:, t0:t1, :, :].rearrange("p t m j -> p (t m j)"),
+                out=w1_codes[z][u][:].bitcast(FP8X4),
+                scales=w1_scales[z][u][:],
+                in_=w1_bf[z][u][:].rearrange("p t m j -> p (t m j)"),
             )
 
-        def cast_wo(engine_copy, b):
-            dst = wo_bf[b][:].rearrange("p (c i) j -> p c j i", i=2)
-            src = wo_raw[b][:].rearrange("p j (c i) -> p c j i", i=2)
+        def cast_wo(engine_copy, b, n0, n1):
+            dst = wo_bf[b][:, n0:n1, :].rearrange("p (c i) j -> p c j i", i=2)
+            src = wo_raw[b][:, :, n0:n1].rearrange("p j (c i) -> p c j i", i=2)
             engine_copy(dst, src)
 
         def quant_wo(b):
@@ -92,27 +97,28 @@ def tile_picked_haar_gelu_p_kernel(tc, x_words, x_scales, w1, w2, w3, offs, out)
                 out=wo_codes[b][:].bitcast(FP8X4), scales=wo_scales[b][:], in_=wo_bf[b][:].rearrange("p n j -> p (n j)")
             )
 
-        def first_product(z, t):
+        def first_product(z, s, d, t, start, stop):
             cols = slice((t % 2) * P, (t % 2 + 1) * P)
+            codes, scales = w1_codes[z][t // 2][:, cols], w1_scales[z][t // 2][:, cols]
+            toks = slice(d * V + s * HALF, d * V + (s + 1) * HALF)
             nc.tensor.matmul_mx(
-                out=pre[t][:],
-                lhsT=w1_codes[z][t // 2][:, cols].bitcast(FP8X4),
-                lhsT_scale=w1_scales[z][t // 2][:, cols],
-                rhs=picked_words[z][:].bitcast(FP4X4),
-                rhs_scale=(picked_scales if z == 0 else moved_scales)[:],
-                start=(z == 0),
-                stop=(z == PASSES - 1),
+                out=pre[s][d][:, t, :],
+                lhsT=codes.bitcast(FP8X4),
+                lhsT_scale=scales,
+                rhs=picked_words[z][:, toks].bitcast(FP4X4),
+                rhs_scale=picked_scales[z][:, toks],
+                start=start,
+                stop=stop,
             )
 
-        def gelu(s, t):
-            src = pre[t][:].rearrange("p (d v) -> p d v", d=2)[:, :, s * HALF : (s + 1) * HALF]
-            nc.scalar.activation(out=hidden[s][:, t, :, :], in_=src, func=GELU)
+        def gelu(s, d, v0, v1):
+            nc.scalar.activation(out=hidden[s][d][:, v0:v1, :], in_=pre[s][d][:, :, v0:v1].rearrange("p t v -> p v t"), func=GELU)
 
-        def band(s, b):
+        def band(s, b, v0, v1):
             nc.vector.tensor_tensor(
-                out=band_bf[s][:, b, :, :].rearrange("p (c i) t -> p c t i", i=2),
-                in0=hidden[s][:, :, 0, :].rearrange("p t (c i) -> p c t i", i=2),
-                in1=hidden[s][:, :, 1, :].rearrange("p t (c i) -> p c t i", i=2),
+                out=band_bf[s][:, b, v0:v1, :],
+                in0=hidden[s][0][:, v0:v1, :],
+                in1=hidden[s][1][:, v0:v1, :],
                 op=(ADD if b == 0 else SUB),
             )
 
@@ -146,63 +152,58 @@ def tile_picked_haar_gelu_p_kernel(tc, x_words, x_scales, w1, w2, w3, offs, out)
             dst = out.rearrange("(mb p) v -> p mb v", p=P)[:, :, s * HALF : (s + 1) * HALF]
             nc.sync.dma_start(out=dst, in_=result[s][:])
 
-        def store_block(queue, s, mb):
-            queue.dma_start(out=out[mb * P : (mb + 1) * P, s * HALF : (s + 1) * HALF], in_=result[s][:, mb, :])
 
         nc.gpsimd.memset(scale_table[:].bitcast(I32), 0)
         nc.vector.memset(warm_in[:], 0.0)
-        nc.vector.memset(moved_scales[:].bitcast(I32), 0)
-        nc.sync.dma_start(out=offsets[:], in_=offs)
+        nc.vector.memset(picked_scales[1][:].bitcast(I32), 0)
         load_words(0)
+        nc.sync.dma_start(out=offsets[:], in_=offs)
         scale_rows = x_scales.rearrange("z (q r) n -> r q z n", r=4)
         for r in range(4):
             nc.sync.dma_start(out=scale_table[r:P:16, :].bitcast(I32), in_=scale_rows[r].bitcast(I32))
         nc.scalar.activation(out=warm_out[:], in_=warm_in[:], func=GELU)
-        load_w1(0, 0)
-        load_w1(0, 1)
-        load_w1(1, 0)
+        load_w1(0)
         load_words(1)
-        load_w1(1, 1)
+        load_w1(1)
 
         nc.vector.tensor_copy(picked_words[0][:], word_table[0][:].indirect(offsets[:]))
-        nc.vector.tensor_copy(picked_scales[:], scale_table[:].indirect(offsets[:]))
+        nc.vector.tensor_copy(picked_scales[0][:], scale_table[:].indirect(offsets[:]))
         for p0, p1 in ((0, 64), (64, 96), (96, 112)):
-            nc.sync.dma_start(out=moved_scales[p0:p1, :].bitcast(I32), in_=picked_scales[p0 + 16 : p1 + 16, :].bitcast(I32))
-        cast_w1(nc.scalar.copy, 0, 0, 0, 4, 0, 64)
+            nc.sync.dma_start(out=picked_scales[1][p0:p1, :].bitcast(I32), in_=picked_scales[0][p0 + 16 : p1 + 16, :].bitcast(I32))
         load_wo(0, w2)
-        cast_w1(nc.vector.tensor_copy, 0, 1, 0, 4, 0, 44)
-        cast_w1(nc.scalar.copy, 0, 1, 0, 4, 44, 64)
+        round_w1(0)
         load_wo(1, w3)
-        quant_w1(0, 0, 2)
-        quant_w1(0, 2, 4)
+        picked_words.append(sb.tile([P, S], U16, name="picked_words1", tag="w1_bf00", align_bytes=64))
         nc.vector.tensor_copy(picked_words[1][:], word_table[1][:].indirect(offsets[:]))
         for t in range(PACK):
-            first_product(0, t)
-        cast_w1(nc.scalar.copy, 1, 0, 0, 4, 0, 64)
-        cast_w1(nc.vector.tensor_copy, 1, 1, 0, 2, 0, 64)
-        cast_w1(nc.scalar.copy, 1, 1, 2, 4, 0, 44)
-        cast_w1(nc.vector.tensor_copy, 1, 1, 2, 4, 44, 64)
-        quant_w1(1, 0, 1)
-        quant_w1(1, 1, 2)
-        quant_w1(1, 2, 4)
+            for s in range(2):
+                for d in range(2):
+                    first_product(0, s, d, t, t == 0, False)
+        round_w1(1)
         for t in range(PACK):
-            first_product(1, t)
-        hidden.append(sb.tile([P, PACK, 2, HALF], F32, name="hidden1", tag="w1_scales11", align_bytes=64))
-        for s in range(2):
-            for t in range(PACK):
-                gelu(s, t)
-        cast_wo(nc.vector.tensor_copy, 0)
-        wo_bf.append(sb.tile([P, N, PACK], BF16, name="w3_bf", tag="w1_codes11", align_bytes=64))
-        cast_wo(nc.scalar.copy, 1)
+            for d in range(2):
+                first_product(1, 0, d, t, False, t == PACK - 1)
+        for d in range(2):
+            for t in reversed(range(PACK)):
+                first_product(1, 1, d, t, False, t == 0)
+        for v0 in (0, 64):
+            gelu(0, 0, v0, v0 + 64)
+            gelu(0, 1, v0, v0 + 64)
+        gelu(1, 0, 0, HALF)
+        gelu(1, 1, 0, HALF)
+        cast_wo(nc.vector.tensor_copy, 0, 0, N)
+        wo_bf.append(sb.tile([P, N, PACK], BF16, name="w3_bf", tag="w1_codes10", align_bytes=64))
+        cast_wo(nc.scalar.copy, 1, 0, N)
         quant_wo(0)
         band_bf.append(sb.tile([P, 2, HALF, PACK], BF16, name="band_bf0", tag="wo_bf0", align_bytes=64))
         band_bf.append(tile([P, 2, HALF, PACK], BF16, "band_bf1"))
-        band(0, 0)
-        band(0, 1)
+        for v0 in (0, 64):
+            band(0, 0, v0, v0 + 64)
+            band(0, 1, v0, v0 + 64)
         quant_band(0, 0)
         quant_band(0, 1)
-        band(1, 0)
-        band(1, 1)
+        band(1, 0, 0, HALF)
+        band(1, 1, 0, HALF)
         quant_band(1, 0)
         quant_wo(1)
         quant_band(1, 1)

@@ -38,7 +38,7 @@ def tile_picked_haar_gelu_p_kernel(tc, x_words, x_scales, w1, w2, w3, offs, out)
         scale_table = tile([P, T], U8, "scale_table")
         picked_scales = [tile([P, S], U8, "picked_scales"), tile([P, S], U8, "moved_scales")]
         word_table = [tile([P, T], U16, "word_table%d" % z) for z in range(PASSES)]
-        picked_words = [tile([P, S], U16, "picked_words0")]
+        picked_words = [tile([P, S], U16, "picked_words%d" % z) for z in range(PASSES)]
         w1_raw = [tile([P, PACK, H], F32, "w1_raw%d" % z) for z in range(PASSES)]
         w1_bf = [[tile([P, 2, P, PACK], BF16, "w1_bf%d%d" % (z, u)) for u in range(2)] for z in range(PASSES)]
         w1_codes = [[tile([P, 2 * P], U32, "w1_codes%d%d" % (z, u)) for u in range(2)] for z in range(PASSES)]
@@ -55,7 +55,22 @@ def tile_picked_haar_gelu_p_kernel(tc, x_words, x_scales, w1, w2, w3, offs, out)
         warm_in = tile([P, 8], F32, "warm_in")
         warm_out = tile([P, 8], F32, "warm_out")
         pre = [[ps.tile([P, PACK, HALF], F32, name="pre%d%d" % (s, d)) for d in range(2)] for s in range(2)]
-        acc = [[ps.tile([P, HALF], F32, name="acc%d%d" % (s, mb)) for mb in range(2)] for s in range(2)]
+        idle_bank = ps.tile([P, S], F32, name="idle_bank")
+        acc = [[ps.tile([P, HALF], F32, name="acc0%d" % mb) for mb in range(2)], [ps.tile([P, HALF], F32, name="acc10")]]
+        zero_bf = tile([P, P * PACK], BF16, "zero_bf")
+        zero_codes = tile([P, P], U32, "zero_codes")
+        zero_scales = tile([P, P], U8, "zero_scales")
+
+        def warm_pass(z, n):
+            nc.tensor.matmul_mx(
+                out=idle_bank[:, 0:n],
+                lhsT=zero_codes[:].bitcast(FP8X4),
+                lhsT_scale=zero_scales[:],
+                rhs=picked_words[z][:, 0:n].bitcast(FP4X4),
+                rhs_scale=picked_scales[0][:, 0:n],
+                start=True,
+                stop=True,
+            )
 
         def load_w1(z):
             rows = w1[z * P * PACK : (z + 1) * P * PACK, :]
@@ -65,7 +80,7 @@ def tile_picked_haar_gelu_p_kernel(tc, x_words, x_scales, w1, w2, w3, offs, out)
             nc.sync.dma_start(out=word_table[z][:].bitcast(I32), in_=x_words[z].bitcast(I32))
 
         def load_wo(b, w):
-            wo_raw.append(sb.tile([P, PACK, N], F32, name="wo_raw%d" % b, tag=("scale_table", "w1_raw0")[b], align_bytes=64))
+            wo_raw.append(sb.tile([P, PACK, N], F32, name="wo_raw%d" % b, tag=("wo_raw0", "scale_table")[b], align_bytes=64))
             nc.sync.dma_start(out=wo_raw[b][:], in_=w.rearrange("(p j) n -> p j n", j=PACK))
 
         def cast_w1(engine_copy, z, u, m0, m1):
@@ -157,42 +172,52 @@ def tile_picked_haar_gelu_p_kernel(tc, x_words, x_scales, w1, w2, w3, offs, out)
         nc.vector.memset(warm_in[:], 0.0)
         nc.vector.memset(picked_scales[1][:].bitcast(I32), 0)
         load_words(0)
+        nc.vector.memset(zero_bf[:], 0.0)
+        nc.vector.quantize_mx(out=zero_codes[:].bitcast(FP8X4), scales=zero_scales[:], in_=zero_bf[:])
         nc.sync.dma_start(out=offsets[:], in_=offs)
+        load_words(1)
         scale_rows = x_scales.rearrange("z (q r) n -> r q z n", r=4)
         for r in range(4):
             nc.sync.dma_start(out=scale_table[r:P:16, :].bitcast(I32), in_=scale_rows[r].bitcast(I32))
         nc.scalar.activation(out=warm_out[:], in_=warm_in[:], func=GELU)
         load_w1(0)
-        load_words(1)
         load_w1(1)
+        load_wo(0, w2)
 
-        nc.vector.tensor_copy(picked_words[0][:], word_table[0][:].indirect(offsets[:]))
+        for z in range(PASSES):
+            nc.vector.tensor_copy(picked_words[z][:], word_table[z][:].indirect(offsets[:]))
         nc.vector.tensor_copy(picked_scales[0][:], scale_table[:].indirect(offsets[:]))
         for p0, p1 in ((0, 64), (64, 96), (96, 112)):
             nc.sync.dma_start(out=picked_scales[1][p0:p1, :].bitcast(I32), in_=picked_scales[0][p0 + 16 : p1 + 16, :].bitcast(I32))
-        load_wo(0, w2)
-        round_w1(0)
+        warm_pass(0, 512)
+        warm_pass(1, 512)
+        acc[1].append(ps.tile([P, HALF], F32, name="acc11", tag="idle_bank"))
         load_wo(1, w3)
-        picked_words.append(sb.tile([P, S], U16, name="picked_words1", tag="w1_bf00", align_bytes=64))
-        nc.vector.tensor_copy(picked_words[1][:], word_table[1][:].indirect(offsets[:]))
+        cast_w1(nc.scalar.copy, 0, 0, 0, P)
+        cast_w1(nc.vector.tensor_copy, 0, 1, 0, 88)
+        cast_w1(nc.scalar.copy, 0, 1, 88, P)
+        quant_w1(0, 0)
+        quant_w1(0, 1)
         for t in range(PACK):
-            for s in range(2):
-                for d in range(2):
-                    first_product(0, s, d, t, t == 0, False)
+            for s, d in ((0, 0), (0, 1), (1, 0)):
+                first_product(0, s, d, t, t == 0, False)
         round_w1(1)
-        for t in range(PACK):
+        for u in range(2):
             for d in range(2):
-                first_product(1, 0, d, t, False, t == PACK - 1)
-        for d in range(2):
+                for t in (2 * u, 2 * u + 1):
+                    first_product(1, 0, d, t, False, t == PACK - 1)
+        for t in reversed(range(PACK)):
+            first_product(1, 1, 0, t, False, t == 0)
+        for z in (1, 0):
             for t in reversed(range(PACK)):
-                first_product(1, 1, d, t, False, t == 0)
+                first_product(z, 1, 1, t, z == 1 and t == PACK - 1, z == 0 and t == 0)
         for v0 in (0, 64):
             gelu(0, 0, v0, v0 + 64)
             gelu(0, 1, v0, v0 + 64)
         gelu(1, 0, 0, HALF)
         gelu(1, 1, 0, HALF)
         cast_wo(nc.vector.tensor_copy, 0, 0, N)
-        wo_bf.append(sb.tile([P, N, PACK], BF16, name="w3_bf", tag="w1_codes10", align_bytes=64))
+        wo_bf.append(sb.tile([P, N, PACK], BF16, name="w3_bf", tag="w1_codes00", align_bytes=64))
         cast_wo(nc.scalar.copy, 1, 0, N)
         quant_wo(0)
         band_bf.append(sb.tile([P, 2, HALF, PACK], BF16, name="band_bf0", tag="wo_bf0", align_bytes=64))
@@ -212,7 +237,7 @@ def tile_picked_haar_gelu_p_kernel(tc, x_words, x_scales, w1, w2, w3, offs, out)
         second_product(0, 1)
         second_product(1, 1)
         halve_on_scalar(0, 0)
-        halve_on_scalar(0, 1)
+        halve_on_vector(0, 1)
         store(0)
         halve_on_scalar(1, 0)
         halve_on_vector(1, 1)

@@ -23,6 +23,10 @@ P = 128
 PACK = 4
 PASSES = K // (P * PACK)
 HALF = V // 2
+QUARTER = HALF // 2
+QUADRANT_ROWS = 4
+SHIFT = 16
+VECTOR_SHARE = (88, 32)
 
 
 def tile_picked_haar_gelu_p_kernel(tc, x_words, x_scales, w1, w2, w3, offs, out):
@@ -34,6 +38,9 @@ def tile_picked_haar_gelu_p_kernel(tc, x_words, x_scales, w1, w2, w3, offs, out)
         def tile(shape, dtype, name):
             return sb.tile(shape, dtype, name=name, align_bytes=64)
 
+        def tile_after(shape, dtype, name, earlier):
+            return sb.tile(shape, dtype, name=name, tag=earlier, align_bytes=64)
+
         offsets = tile([P, S // 16], U16, "offsets")
         scale_table = tile([P, T], U8, "scale_table")
         picked_scales = [tile([P, S], U8, "picked_scales"), tile([P, S], U8, "moved_scales")]
@@ -43,85 +50,75 @@ def tile_picked_haar_gelu_p_kernel(tc, x_words, x_scales, w1, w2, w3, offs, out)
         w1_bf = [[tile([P, 2, P, PACK], BF16, "w1_bf%d%d" % (z, u)) for u in range(2)] for z in range(PASSES)]
         w1_codes = [[tile([P, 2 * P], U32, "w1_codes%d%d" % (z, u)) for u in range(2)] for z in range(PASSES)]
         w1_scales = [[tile([P, 2 * P], U8, "w1_scales%d%d" % (z, u)) for u in range(2)] for z in range(PASSES)]
-        wo_raw = []
         wo_bf = [tile([P, N, PACK], BF16, "wo_bf0")]
         wo_codes = [tile([P, N], U32, "wo_codes%d" % b) for b in range(2)]
         wo_scales = [tile([P, N], U8, "wo_scales%d" % b) for b in range(2)]
         hidden = [[tile([P, HALF, PACK], F32, "hidden%d%d" % (s, d)) for d in range(2)] for s in range(2)]
-        band_bf = []
         band_codes = [[tile([P, HALF], U32, "band_codes%d%d" % (s, b)) for b in range(2)] for s in range(2)]
         band_scales = [[tile([P, HALF], U8, "band_scales%d%d" % (s, b)) for b in range(2)] for s in range(2)]
         result = [tile([P, 2, HALF], F32, "result%d" % s) for s in range(2)]
-        warm_in = tile([P, 8], F32, "warm_in")
-        warm_out = tile([P, 8], F32, "warm_out")
+        preload_out = tile([P, 8], F32, "preload_out")
         pre = [[ps.tile([P, PACK, HALF], F32, name="pre%d%d" % (s, d)) for d in range(2)] for s in range(2)]
-        idle_bank = ps.tile([P, S], F32, name="idle_bank")
+        warm_bank = ps.tile([P, S], F32, name="warm_bank")
         acc = [[ps.tile([P, HALF], F32, name="acc0%d" % mb) for mb in range(2)], [ps.tile([P, HALF], F32, name="acc10")]]
         zero_bf = tile([P, P * PACK], BF16, "zero_bf")
         zero_codes = tile([P, P], U32, "zero_codes")
         zero_scales = tile([P, P], U8, "zero_scales")
+        wo_raw = []
+        band_bf = []
 
-        def warm_pass(z, n):
-            nc.tensor.matmul_mx(
-                out=idle_bank[:, 0:n],
-                lhsT=zero_codes[:].bitcast(FP8X4),
-                lhsT_scale=zero_scales[:],
-                rhs=picked_words[z][:, 0:n].bitcast(FP4X4),
-                rhs_scale=picked_scales[0][:, 0:n],
-                start=True,
-                stop=True,
-            )
+        def load_words(z):
+            nc.sync.dma_start(out=word_table[z][:].bitcast(I32), in_=x_words[z].bitcast(I32))
 
         def load_w1(z):
             rows = w1[z * P * PACK : (z + 1) * P * PACK, :]
             nc.sync.dma_start(out=w1_raw[z][:], in_=rows.rearrange("(p j) n -> p j n", j=PACK))
 
-        def load_words(z):
-            nc.sync.dma_start(out=word_table[z][:].bitcast(I32), in_=x_words[z].bitcast(I32))
-
         def load_wo(b, w):
-            wo_raw.append(sb.tile([P, PACK, N], F32, name="wo_raw%d" % b, tag=("wo_raw0", "scale_table")[b], align_bytes=64))
             nc.sync.dma_start(out=wo_raw[b][:], in_=w.rearrange("(p j) n -> p j n", j=PACK))
 
-        def cast_w1(engine_copy, z, u, m0, m1):
+        def round_w1(engine_copy, z, u, m0, m1):
             dst = w1_bf[z][u][:, :, m0:m1, :].rearrange("p t m j -> p m j t")
             src = w1_raw[z][:, :, PACK * m0 : PACK * m1].rearrange("p j (m t) -> p m j t", t=PACK)
             engine_copy(dst, src[:, :, :, 2 * u : 2 * u + 2])
 
-        def round_w1(z):
-            cast_w1(nc.vector.tensor_copy, z, 0, 0, P)
-            cast_w1(nc.scalar.copy, z, 1, 32, P)
-            cast_w1(nc.vector.tensor_copy, z, 1, 0, 32)
-            quant_w1(z, 0)
-            quant_w1(z, 1)
-
-        def quant_w1(z, u):
+        def quantise_w1(z, u):
             nc.vector.quantize_mx(
                 out=w1_codes[z][u][:].bitcast(FP8X4),
                 scales=w1_scales[z][u][:],
                 in_=w1_bf[z][u][:].rearrange("p t m j -> p (t m j)"),
             )
 
-        def cast_wo(engine_copy, b, n0, n1):
-            dst = wo_bf[b][:, n0:n1, :].rearrange("p (c i) j -> p c j i", i=2)
-            src = wo_raw[b][:, :, n0:n1].rearrange("p j (c i) -> p c j i", i=2)
+        def round_wo(engine_copy, b):
+            dst = wo_bf[b][:].rearrange("p (c i) j -> p c j i", i=2)
+            src = wo_raw[b][:].rearrange("p j (c i) -> p c j i", i=2)
             engine_copy(dst, src)
 
-        def quant_wo(b):
+        def quantise_wo(b):
             nc.vector.quantize_mx(
                 out=wo_codes[b][:].bitcast(FP8X4), scales=wo_scales[b][:], in_=wo_bf[b][:].rearrange("p n j -> p (n j)")
             )
 
+        def warm_up(z):
+            nc.tensor.matmul_mx(
+                out=warm_bank[:],
+                lhsT=zero_codes[:].bitcast(FP8X4),
+                lhsT_scale=zero_scales[:],
+                rhs=picked_words[z][:].bitcast(FP4X4),
+                rhs_scale=picked_scales[0][:],
+                start=True,
+                stop=True,
+            )
+
         def first_product(z, s, d, t, start, stop):
             cols = slice((t % 2) * P, (t % 2 + 1) * P)
-            codes, scales = w1_codes[z][t // 2][:, cols], w1_scales[z][t // 2][:, cols]
-            toks = slice(d * V + s * HALF, d * V + (s + 1) * HALF)
+            entries = slice(d * V + s * HALF, d * V + (s + 1) * HALF)
             nc.tensor.matmul_mx(
                 out=pre[s][d][:, t, :],
-                lhsT=codes.bitcast(FP8X4),
-                lhsT_scale=scales,
-                rhs=picked_words[z][:, toks].bitcast(FP4X4),
-                rhs_scale=picked_scales[z][:, toks],
+                lhsT=w1_codes[z][t // 2][:, cols].bitcast(FP8X4),
+                lhsT_scale=w1_scales[z][t // 2][:, cols],
+                rhs=picked_words[z][:, entries].bitcast(FP4X4),
+                rhs_scale=picked_scales[z][:, entries],
                 start=start,
                 stop=stop,
             )
@@ -137,7 +134,7 @@ def tile_picked_haar_gelu_p_kernel(tc, x_words, x_scales, w1, w2, w3, offs, out)
                 op=(ADD if b == 0 else SUB),
             )
 
-        def quant_band(s, b):
+        def quantise_band(s, b):
             nc.vector.quantize_mx(
                 out=band_codes[s][b][:].bitcast(FP8X4),
                 scales=band_scales[s][b][:],
@@ -157,88 +154,93 @@ def tile_picked_haar_gelu_p_kernel(tc, x_words, x_scales, w1, w2, w3, offs, out)
                     stop=(b == 1),
                 )
 
-        def halve_on_scalar(s, mb):
-            nc.scalar.activation(out=result[s][:, mb, :], in_=acc[s][mb][:], func=COPY, scale=0.5)
-
-        def halve_on_vector(s, mb):
-            nc.vector.tensor_scalar(out=result[s][:, mb, :], in0=acc[s][mb][:], scalar1=0.5, scalar2=None, op0=MULT)
-
-        def store(s):
+        def halve_and_store(s):
+            nc.scalar.activation(out=result[s][:, 0, :], in_=acc[s][0][:], func=COPY, scale=0.5)
+            nc.vector.tensor_scalar(out=result[s][:, 1, :], in0=acc[s][1][:], scalar1=0.5, scalar2=None, op0=MULT)
             dst = out.rearrange("(mb p) v -> p mb v", p=P)[:, :, s * HALF : (s + 1) * HALF]
             nc.sync.dma_start(out=dst, in_=result[s][:])
 
-
         nc.gpsimd.memset(scale_table[:].bitcast(I32), 0)
-        nc.vector.memset(warm_in[:], 0.0)
+        nc.vector.memset(zero_bf[:].bitcast(I32), 0)
         nc.vector.memset(picked_scales[1][:].bitcast(I32), 0)
-        load_words(0)
-        nc.vector.memset(zero_bf[:], 0.0)
         nc.vector.quantize_mx(out=zero_codes[:].bitcast(FP8X4), scales=zero_scales[:], in_=zero_bf[:])
+
+        load_words(0)
         nc.sync.dma_start(out=offsets[:], in_=offs)
         load_words(1)
-        scale_rows = x_scales.rearrange("z (q r) n -> r q z n", r=4)
-        for r in range(4):
-            nc.sync.dma_start(out=scale_table[r:P:16, :].bitcast(I32), in_=scale_rows[r].bitcast(I32))
-        nc.scalar.activation(out=warm_out[:], in_=warm_in[:], func=GELU)
+        scale_rows = x_scales.rearrange("z (q r) n -> r q z n", r=QUADRANT_ROWS)
+        for r in range(QUADRANT_ROWS):
+            nc.sync.dma_start(out=scale_table[r:P:SHIFT, :].bitcast(I32), in_=scale_rows[r].bitcast(I32))
+        nc.scalar.activation(out=preload_out[:], in_=zero_bf[:, 0:8], func=GELU)
         load_w1(0)
         load_w1(1)
+        wo_raw.append(tile([P, PACK, N], F32, "wo_raw0"))
         load_wo(0, w2)
 
         for z in range(PASSES):
             nc.vector.tensor_copy(picked_words[z][:], word_table[z][:].indirect(offsets[:]))
         nc.vector.tensor_copy(picked_scales[0][:], scale_table[:].indirect(offsets[:]))
-        for p0, p1 in ((0, 64), (64, 96), (96, 112)):
-            nc.sync.dma_start(out=picked_scales[1][p0:p1, :].bitcast(I32), in_=picked_scales[0][p0 + 16 : p1 + 16, :].bitcast(I32))
-        warm_pass(0, 512)
-        warm_pass(1, 512)
-        acc[1].append(ps.tile([P, HALF], F32, name="acc11", tag="idle_bank"))
+        for p0, p1 in ((0, 64), (64, 96), (96, P - SHIFT)):
+            nc.sync.dma_start(
+                out=picked_scales[1][p0:p1, :].bitcast(I32), in_=picked_scales[0][p0 + SHIFT : p1 + SHIFT, :].bitcast(I32)
+            )
+        for z in range(PASSES):
+            warm_up(z)
+        acc[1].append(ps.tile([P, HALF], F32, name="acc11", tag="warm_bank"))
+        wo_raw.append(tile_after([P, PACK, N], F32, "wo_raw1", "scale_table"))
         load_wo(1, w3)
-        cast_w1(nc.scalar.copy, 0, 0, 0, P)
-        cast_w1(nc.vector.tensor_copy, 0, 1, 0, 88)
-        cast_w1(nc.scalar.copy, 0, 1, 88, P)
-        quant_w1(0, 0)
-        quant_w1(0, 1)
+
+        round_w1(nc.scalar.copy, 0, 0, 0, P)
+        round_w1(nc.vector.tensor_copy, 0, 1, 0, VECTOR_SHARE[0])
+        round_w1(nc.scalar.copy, 0, 1, VECTOR_SHARE[0], P)
+        for u in range(2):
+            quantise_w1(0, u)
         for t in range(PACK):
-            for s, d in ((0, 0), (0, 1), (1, 0)):
-                first_product(0, s, d, t, t == 0, False)
-        round_w1(1)
+            for d in range(2):
+                first_product(0, 0, d, t, t == 0, False)
+
+        round_w1(nc.vector.tensor_copy, 1, 0, 0, P)
+        round_w1(nc.scalar.copy, 1, 1, VECTOR_SHARE[1], P)
+        round_w1(nc.vector.tensor_copy, 1, 1, 0, VECTOR_SHARE[1])
+        for u in range(2):
+            quantise_w1(1, u)
         for u in range(2):
             for d in range(2):
                 for t in (2 * u, 2 * u + 1):
                     first_product(1, 0, d, t, False, t == PACK - 1)
-        for t in reversed(range(PACK)):
-            first_product(1, 1, 0, t, False, t == 0)
-        for z in (1, 0):
-            for t in reversed(range(PACK)):
-                first_product(z, 1, 1, t, z == 1 and t == PACK - 1, z == 0 and t == 0)
-        for v0 in (0, 64):
-            gelu(0, 0, v0, v0 + 64)
-            gelu(0, 1, v0, v0 + 64)
+        for d in range(2):
+            for z in reversed(range(PASSES)):
+                for t in reversed(range(PACK)):
+                    first_product(z, 1, d, t, z == PASSES - 1 and t == PACK - 1, z == 0 and t == 0)
+
+        for v0 in (0, QUARTER):
+            for d in range(2):
+                gelu(0, d, v0, v0 + QUARTER)
         gelu(1, 0, 0, HALF)
-        gelu(1, 1, 0, HALF)
-        cast_wo(nc.vector.tensor_copy, 0, 0, N)
-        wo_bf.append(sb.tile([P, N, PACK], BF16, name="w3_bf", tag="w1_codes00", align_bytes=64))
-        cast_wo(nc.scalar.copy, 1, 0, N)
-        quant_wo(0)
-        band_bf.append(sb.tile([P, 2, HALF, PACK], BF16, name="band_bf0", tag="wo_bf0", align_bytes=64))
+        for v0 in (0, QUARTER):
+            gelu(1, 1, v0, v0 + QUARTER)
+
+        round_wo(nc.vector.tensor_copy, 0)
+        wo_bf.append(tile_after([P, N, PACK], BF16, "wo_bf1", "w1_codes00"))
+        round_wo(nc.scalar.copy, 1)
+        quantise_wo(0)
+
+        band_bf.append(tile_after([P, 2, HALF, PACK], BF16, "band_bf0", "wo_bf0"))
         band_bf.append(tile([P, 2, HALF, PACK], BF16, "band_bf1"))
-        for v0 in (0, 64):
-            band(0, 0, v0, v0 + 64)
-            band(0, 1, v0, v0 + 64)
-        quant_band(0, 0)
-        quant_band(0, 1)
-        band(1, 0, 0, HALF)
+        for v0 in (0, QUARTER):
+            for b in range(2):
+                band(0, b, v0, v0 + QUARTER)
+        for b in range(2):
+            quantise_band(0, b)
+        for v0 in (0, QUARTER):
+            band(1, 0, v0, v0 + QUARTER)
         band(1, 1, 0, HALF)
-        quant_band(1, 0)
-        quant_wo(1)
-        quant_band(1, 1)
-        second_product(0, 0)
-        second_product(1, 0)
-        second_product(0, 1)
-        second_product(1, 1)
-        halve_on_scalar(0, 0)
-        halve_on_vector(0, 1)
-        store(0)
-        halve_on_scalar(1, 0)
-        halve_on_vector(1, 1)
-        store(1)
+        quantise_band(1, 0)
+        quantise_wo(1)
+        quantise_band(1, 1)
+
+        for b in range(2):
+            for s in range(2):
+                second_product(s, b)
+        for s in range(2):
+            halve_and_store(s)

@@ -53,7 +53,8 @@ def tile_picked_haar_gelu_p_kernel(tc, x_words, x_scales, w1, w2, w3, offs, out)
         wo_bf = [tile([P, N, PACK], BF16, "wo_bf0")]
         wo_codes = [tile([P, N], U32, "wo_codes%d" % b) for b in range(2)]
         wo_scales = [tile([P, N], U8, "wo_scales%d" % b) for b in range(2)]
-        hidden = [[tile([P, HALF, PACK], F32, "hidden%d%d" % (s, d)) for d in range(2)] for s in range(2)]
+        hidden_first = tile([P, 2, 2, HALF, 2], F32, "hidden0")
+        hidden = [None, [tile([P, HALF, PACK], F32, "hidden1%d" % d) for d in range(2)]]
         band_codes = [[tile([P, HALF], U32, "band_codes%d%d" % (s, b)) for b in range(2)] for s in range(2)]
         band_scales = [[tile([P, HALF], U8, "band_scales%d%d" % (s, b)) for b in range(2)] for s in range(2)]
         result = [tile([P, 2, HALF], F32, "result%d" % s) for s in range(2)]
@@ -89,9 +90,9 @@ def tile_picked_haar_gelu_p_kernel(tc, x_words, x_scales, w1, w2, w3, offs, out)
                 in_=w1_bf[z][u][:].rearrange("p t m j -> p (t m j)"),
             )
 
-        def round_wo(engine_copy, b):
-            dst = wo_bf[b][:].rearrange("p (c i) j -> p c j i", i=2)
-            src = wo_raw[b][:].rearrange("p j (c i) -> p c j i", i=2)
+        def round_wo(engine_copy, b, n0, n1):
+            dst = wo_bf[b][:, n0:n1, :].rearrange("p (c i) j -> p c j i", i=4)
+            src = wo_raw[b][:, :, n0:n1].rearrange("p j (c i) -> p c j i", i=4)
             engine_copy(dst, src)
 
         def quantise_wo(b):
@@ -114,7 +115,7 @@ def tile_picked_haar_gelu_p_kernel(tc, x_words, x_scales, w1, w2, w3, offs, out)
             cols = slice((t % 2) * P, (t % 2 + 1) * P)
             entries = slice(d * V + s * HALF, d * V + (s + 1) * HALF)
             nc.tensor.matmul_mx(
-                out=pre[s][d][:, t, :],
+                out=(pre[0][t // 2][:, 2 * d + t % 2, :] if s == 0 else pre[s][d][:, t, :]),
                 lhsT=w1_codes[z][t // 2][:, cols].bitcast(FP8X4),
                 lhsT_scale=w1_scales[z][t // 2][:, cols],
                 rhs=picked_words[z][:, entries].bitcast(FP4X4),
@@ -125,6 +126,18 @@ def tile_picked_haar_gelu_p_kernel(tc, x_words, x_scales, w1, w2, w3, offs, out)
 
         def gelu(s, d, v0, v1):
             nc.scalar.activation(out=hidden[s][d][:, v0:v1, :], in_=pre[s][d][:, :, v0:v1].rearrange("p t v -> p v t"), func=GELU)
+
+        def gelu_first(u, v0, v1):
+            src = pre[0][u][:, :, v0:v1].rearrange("p (d t) v -> p d v t", d=2)
+            nc.scalar.activation(out=hidden_first[:, u, :, v0:v1, :], in_=src, func=GELU)
+
+        def band_first(b, v0, v1):
+            nc.vector.tensor_tensor(
+                out=band_bf[0][:, b, v0:v1, :].rearrange("p v (u t) -> p v u t", u=2),
+                in0=hidden_first[:, :, 0, v0:v1, :].rearrange("p u v t -> p v u t"),
+                in1=hidden_first[:, :, 1, v0:v1, :].rearrange("p u v t -> p v u t"),
+                op=(ADD if b == 0 else SUB),
+            )
 
         def band(s, b, v0, v1):
             nc.vector.tensor_tensor(
@@ -197,7 +210,7 @@ def tile_picked_haar_gelu_p_kernel(tc, x_words, x_scales, w1, w2, w3, offs, out)
             quantise_w1(0, u)
         for t in range(PACK):
             for d in range(2):
-                first_product(0, 0, d, t, t == 0, False)
+                first_product(0, 0, d, t, t % 2 == 0 and d == 0, False)
 
         round_w1(nc.vector.tensor_copy, 1, 0, 0, P)
         round_w1(nc.scalar.copy, 1, 1, VECTOR_SHARE[1], P)
@@ -207,34 +220,36 @@ def tile_picked_haar_gelu_p_kernel(tc, x_words, x_scales, w1, w2, w3, offs, out)
         for u in range(2):
             for d in range(2):
                 for t in (2 * u, 2 * u + 1):
-                    first_product(1, 0, d, t, False, t == PACK - 1)
+                    first_product(1, 0, d, t, False, d == 1 and t % 2 == 1)
         for d in range(2):
             for z in reversed(range(PASSES)):
                 for t in reversed(range(PACK)):
                     first_product(z, 1, d, t, z == PASSES - 1 and t == PACK - 1, z == 0 and t == 0)
 
-        for v0 in (0, QUARTER):
-            for d in range(2):
-                gelu(0, d, v0, v0 + QUARTER)
+        round_wo(nc.scalar.copy, 0, 0, 128)
+        gelu_first(0, 0, HALF)
+        for v0, v1 in ((0, 32), (32, HALF)):
+            gelu_first(1, v0, v1)
         gelu(1, 0, 0, HALF)
-        for v0 in (0, QUARTER):
-            gelu(1, 1, v0, v0 + QUARTER)
+        for v0, v1 in ((0, 96), (96, HALF)):
+            gelu(1, 1, v0, v1)
 
-        round_wo(nc.vector.tensor_copy, 0)
+        round_wo(nc.vector.tensor_copy, 0, 128, N)
         wo_bf.append(tile_after([P, N, PACK], BF16, "wo_bf1", "w1_codes00"))
-        round_wo(nc.scalar.copy, 1)
+        round_wo(nc.vector.tensor_copy, 1, 0, 16)
+        round_wo(nc.scalar.copy, 1, 16, N)
         quantise_wo(0)
 
-        band_bf.append(tile_after([P, 2, HALF, PACK], BF16, "band_bf0", "wo_bf0"))
+        band_bf.append(tile([P, 2, HALF, PACK], BF16, "band_bf0"))
         band_bf.append(tile([P, 2, HALF, PACK], BF16, "band_bf1"))
-        for v0 in (0, QUARTER):
+        for v0, v1 in ((0, 32), (32, HALF)):
             for b in range(2):
-                band(0, b, v0, v0 + QUARTER)
+                band_first(b, v0, v1)
         for b in range(2):
             quantise_band(0, b)
-        for v0 in (0, QUARTER):
-            band(1, 0, v0, v0 + QUARTER)
-        band(1, 1, 0, HALF)
+        for v0, v1 in ((0, 96), (96, HALF)):
+            for b in range(2):
+                band(1, b, v0, v1)
         quantise_band(1, 0)
         quantise_wo(1)
         quantise_band(1, 1)

@@ -46,7 +46,8 @@ def tile_picked_haar_gelu_p_kernel(tc, x_words, x_scales, w1, w2, w3, offs, out)
         picked_scales = [tile([P, S], U8, "picked_scales"), tile([P, S], U8, "moved_scales")]
         word_table = [tile([P, T], U16, "word_table%d" % z) for z in range(PASSES)]
         picked_words = [tile([P, S], U16, "picked_words%d" % z) for z in range(PASSES)]
-        w1_raw = [tile([P, PACK, H], F32, "w1_raw%d" % z) for z in range(PASSES)]
+        w1_raw = [tile([P, PACK, H], F32, "w1_raw0")]
+        w1_late = [tile([P, 2, H], F32, "w1_late%d" % h) for h in range(2)]
         w1_bf = [[tile([P, 2, P, PACK], BF16, "w1_bf%d%d" % (z, u)) for u in range(2)] for z in range(PASSES)]
         w1_codes = [[tile([P, 2 * P], U32, "w1_codes%d%d" % (z, u)) for u in range(2)] for z in range(PASSES)]
         w1_scales = [[tile([P, 2 * P], U8, "w1_scales%d%d" % (z, u)) for u in range(2)] for z in range(PASSES)]
@@ -77,6 +78,28 @@ def tile_picked_haar_gelu_p_kernel(tc, x_words, x_scales, w1, w2, w3, offs, out)
 
         def load_wo(b, w):
             nc.sync.dma_start(out=wo_raw[b][:], in_=w.rearrange("(p j) n -> p j n", j=PACK))
+
+        def load_w2(h):
+            nc.sync.dma_start(out=w2_raw[h][:], in_=w2.rearrange("(p j) n -> p j n", j=PACK)[:, 2 * h : 2 * h + 2, :])
+
+        def round_w2(engine_copy, h):
+            dst = wo_bf[0][:, :, 2 * h : 2 * h + 2].rearrange("p (c i) j -> p c j i", i=4)
+            src = w2_raw[h][:].rearrange("p j (c i) -> p c j i", i=4)
+            engine_copy(dst, src)
+
+        def load_w1_late(h):
+            rows = w1[P * PACK :, :].rearrange("(p j) n -> p j n", j=PACK)
+            nc.sync.dma_start(out=w1_late[h][:], in_=rows[:, 2 * h : 2 * h + 2, :])
+
+        def round_late_pair(engine_copy, h, u):
+            dst = w1_bf[1][u][:, :, :, 2 * h : 2 * h + 2].rearrange("p t m j -> p m j t")
+            src = w1_late[h][:].rearrange("p j (m t) -> p m j t", t=PACK)
+            engine_copy(dst, src[:, :, :, 2 * u : 2 * u + 2])
+
+        def round_late_slot(engine_copy, h, t, m0, m1):
+            dst = w1_bf[1][t // 2][:, t % 2, m0:m1, 2 * h : 2 * h + 2]
+            src = w1_late[h][:].rearrange("p j (m t) -> p m j t", t=PACK)
+            engine_copy(dst, src[:, m0:m1, :, t])
 
         def round_w1(engine_copy, z, u, m0, m1):
             dst = w1_bf[z][u][:, :, m0:m1, :].rearrange("p t m j -> p m j t")
@@ -186,21 +209,25 @@ def tile_picked_haar_gelu_p_kernel(tc, x_words, x_scales, w1, w2, w3, offs, out)
             nc.sync.dma_start(out=scale_table[r:P:SHIFT, :].bitcast(I32), in_=scale_rows[r].bitcast(I32))
         nc.scalar.activation(out=preload_out[:], in_=zero_bf[:, 0:8], func=GELU)
         load_w1(0)
-        load_w1(1)
-        wo_raw.append(tile([P, PACK, N], F32, "wo_raw0"))
-        load_wo(0, w2)
+        for h in range(2):
+            load_w1_late(h)
+        wo_raw.append(None)
+        w2_raw = [tile([P, 2, N], F32, "w2_raw0")]
+        load_w2(0)
 
         for z in range(PASSES):
             nc.vector.tensor_copy(picked_words[z][:], word_table[z][:].indirect(offsets[:]))
         nc.vector.tensor_copy(picked_scales[0][:], scale_table[:].indirect(offsets[:]))
-        for p0, p1 in ((0, 64), (64, 96), (96, P - SHIFT)):
+        for p0, p1 in ((0, P - SHIFT),):
             nc.sync.dma_start(
                 out=picked_scales[1][p0:p1, :].bitcast(I32), in_=picked_scales[0][p0 + SHIFT : p1 + SHIFT, :].bitcast(I32)
             )
         for z in range(PASSES):
             warm_up(z)
         acc[1].append(ps.tile([P, HALF], F32, name="acc11", tag="warm_bank"))
-        wo_raw.append(tile_after([P, PACK, N], F32, "wo_raw1", "scale_table"))
+        w2_raw.append(tile_after([P, 2, N], F32, "w2_raw1", "scale_table"))
+        load_w2(1)
+        wo_raw.append(tile_after([P, PACK, N], F32, "wo_raw1", "w1_raw0"))
         load_wo(1, w3)
 
         round_w1(nc.scalar.copy, 0, 0, 0, P)
@@ -212,9 +239,12 @@ def tile_picked_haar_gelu_p_kernel(tc, x_words, x_scales, w1, w2, w3, offs, out)
             for d in range(2):
                 first_product(0, 0, d, t, t % 2 == 0 and d == 0, False)
 
-        round_w1(nc.vector.tensor_copy, 1, 0, 0, P)
-        round_w1(nc.scalar.copy, 1, 1, VECTOR_SHARE[1], P)
-        round_w1(nc.vector.tensor_copy, 1, 1, 0, VECTOR_SHARE[1])
+        round_late_pair(nc.vector.tensor_copy, 0, 0)
+        round_late_pair(nc.scalar.copy, 0, 1)
+        round_late_pair(nc.vector.tensor_copy, 1, 0)
+        round_late_slot(nc.scalar.copy, 1, 3, 0, P)
+        round_late_slot(nc.vector.tensor_copy, 1, 2, 0, 64)
+        round_late_slot(nc.scalar.copy, 1, 2, 64, P)
         for u in range(2):
             quantise_w1(1, u)
         for u in range(2):
@@ -226,7 +256,7 @@ def tile_picked_haar_gelu_p_kernel(tc, x_words, x_scales, w1, w2, w3, offs, out)
                 for t in reversed(range(PACK)):
                     first_product(z, 1, d, t, z == PASSES - 1 and t == PACK - 1, z == 0 and t == 0)
 
-        round_wo(nc.scalar.copy, 0, 0, 128)
+        round_w2(nc.scalar.copy, 0)
         gelu_first(0, 0, HALF)
         for v0, v1 in ((0, 32), (32, HALF)):
             gelu_first(1, v0, v1)
@@ -234,7 +264,7 @@ def tile_picked_haar_gelu_p_kernel(tc, x_words, x_scales, w1, w2, w3, offs, out)
         for v0, v1 in ((0, 96), (96, HALF)):
             gelu(1, 1, v0, v1)
 
-        round_wo(nc.vector.tensor_copy, 0, 128, N)
+        round_w2(nc.vector.tensor_copy, 1)
         wo_bf.append(tile_after([P, N, PACK], BF16, "wo_bf1", "w1_codes00"))
         round_wo(nc.vector.tensor_copy, 1, 0, 16)
         round_wo(nc.scalar.copy, 1, 16, N)

@@ -91,15 +91,10 @@ def tile_picked_haar_gelu_p_kernel(tc, x_words, x_scales, w1, w2, w3, offs, out)
             rows = w1[P * PACK :, :].rearrange("(p j) n -> p j n", j=PACK)
             nc.sync.dma_start(out=w1_late[h][:], in_=rows[:, 2 * h : 2 * h + 2, :])
 
-        def round_late_pair(engine_copy, h, u):
-            dst = w1_bf[1][u][:, :, :, 2 * h : 2 * h + 2].rearrange("p t m j -> p m j t")
+        def round_late_pair(engine_copy, h, u, m0, m1):
+            dst = w1_bf[1][u][:, :, m0:m1, 2 * h : 2 * h + 2].rearrange("p t m j -> p m j t")
             src = w1_late[h][:].rearrange("p j (m t) -> p m j t", t=PACK)
-            engine_copy(dst, src[:, :, :, 2 * u : 2 * u + 2])
-
-        def round_late_slot(engine_copy, h, t, m0, m1):
-            dst = w1_bf[1][t // 2][:, t % 2, m0:m1, 2 * h : 2 * h + 2]
-            src = w1_late[h][:].rearrange("p j (m t) -> p m j t", t=PACK)
-            engine_copy(dst, src[:, m0:m1, :, t])
+            engine_copy(dst, src[:, m0:m1, :, 2 * u : 2 * u + 2])
 
         def round_w1(engine_copy, z, u, m0, m1):
             dst = w1_bf[z][u][:, :, m0:m1, :].rearrange("p t m j -> p m j t")
@@ -239,12 +234,11 @@ def tile_picked_haar_gelu_p_kernel(tc, x_words, x_scales, w1, w2, w3, offs, out)
             for d in range(2):
                 first_product(0, 0, d, t, t % 2 == 0 and d == 0, False)
 
-        round_late_pair(nc.vector.tensor_copy, 0, 0)
-        round_late_pair(nc.scalar.copy, 0, 1)
-        round_late_pair(nc.vector.tensor_copy, 1, 0)
-        round_late_slot(nc.scalar.copy, 1, 3, 0, P)
-        round_late_slot(nc.vector.tensor_copy, 1, 2, 0, 64)
-        round_late_slot(nc.scalar.copy, 1, 2, 64, P)
+        round_late_pair(nc.vector.tensor_copy, 0, 0, 0, P)
+        round_late_pair(nc.scalar.copy, 0, 1, 0, P)
+        round_late_pair(nc.vector.tensor_copy, 1, 0, 0, P)
+        round_late_pair(nc.scalar.copy, 1, 1, 40, P)
+        round_late_pair(nc.vector.tensor_copy, 1, 1, 0, 40)
         for u in range(2):
             quantise_w1(1, u)
         for u in range(2):

@@ -23,10 +23,13 @@ P = 128
 PACK = 4
 PASSES = K // (P * PACK)
 HALF = V // 2
-QUARTER = HALF // 2
 QUADRANT_ROWS = 4
 SHIFT = 16
-VECTOR_SHARE = (88, 32)
+LINE = 4
+VECTOR_SHARE_PASS0 = 88
+VECTOR_SHARE_LAST = 40
+FIRST_PIECES = ((0, 32), (32, 64), (64, HALF))
+SECOND_PIECES = ((0, 96), (96, HALF))
 
 
 def tile_picked_haar_gelu_p_kernel(tc, x_words, x_scales, w1, w2, w3, offs, out):
@@ -46,76 +49,55 @@ def tile_picked_haar_gelu_p_kernel(tc, x_words, x_scales, w1, w2, w3, offs, out)
         picked_scales = [tile([P, S], U8, "picked_scales"), tile([P, S], U8, "moved_scales")]
         word_table = [tile([P, T], U16, "word_table%d" % z) for z in range(PASSES)]
         picked_words = [tile([P, S], U16, "picked_words%d" % z) for z in range(PASSES)]
-        w1_raw = [tile([P, PACK, H], F32, "w1_raw0")]
-        w1_late = [tile([P, 2, H], F32, "w1_late%d" % h) for h in range(2)]
+        pass0_raw = tile([P, PACK, H], F32, "pass0_raw")
+        pass1_raw = [tile([P, 2, H], F32, "pass1_raw%d" % h) for h in range(2)]
         w1_bf = [[tile([P, 2, P, PACK], BF16, "w1_bf%d%d" % (z, u)) for u in range(2)] for z in range(PASSES)]
         w1_codes = [[tile([P, 2 * P], U32, "w1_codes%d%d" % (z, u)) for u in range(2)] for z in range(PASSES)]
         w1_scales = [[tile([P, 2 * P], U8, "w1_scales%d%d" % (z, u)) for u in range(2)] for z in range(PASSES)]
-        wo_bf = [tile([P, N, PACK], BF16, "wo_bf0")]
+        w2_bf = tile([P, N, PACK], BF16, "w2_bf")
         wo_codes = [tile([P, N], U32, "wo_codes%d" % b) for b in range(2)]
         wo_scales = [tile([P, N], U8, "wo_scales%d" % b) for b in range(2)]
-        hidden_first = tile([P, 2, 2, HALF, 2], F32, "hidden0")
-        hidden = [None, [tile([P, HALF, PACK], F32, "hidden1%d" % d) for d in range(2)]]
+        hidden_first = tile([P, 2, 2, HALF, 2], F32, "hidden_first")
+        hidden_second = [tile([P, HALF, PACK], F32, "hidden_second%d" % d) for d in range(2)]
         band_codes = [[tile([P, HALF], U32, "band_codes%d%d" % (s, b)) for b in range(2)] for s in range(2)]
         band_scales = [[tile([P, HALF], U8, "band_scales%d%d" % (s, b)) for b in range(2)] for s in range(2)]
         result = [tile([P, 2, HALF], F32, "result%d" % s) for s in range(2)]
         preload_out = tile([P, 8], F32, "preload_out")
-        pre = [[ps.tile([P, PACK, HALF], F32, name="pre%d%d" % (s, d)) for d in range(2)] for s in range(2)]
+        pre_first = [ps.tile([P, PACK, HALF], F32, name="pre_first%d" % u) for u in range(2)]
+        pre_second = [ps.tile([P, PACK, HALF], F32, name="pre_second%d" % d) for d in range(2)]
         warm_bank = ps.tile([P, S], F32, name="warm_bank")
         acc = [[ps.tile([P, HALF], F32, name="acc0%d" % mb) for mb in range(2)], [ps.tile([P, HALF], F32, name="acc10")]]
         zero_bf = tile([P, P * PACK], BF16, "zero_bf")
         zero_codes = tile([P, P], U32, "zero_codes")
         zero_scales = tile([P, P], U8, "zero_scales")
-        wo_raw = []
-        band_bf = []
 
         def load_words(z):
             nc.sync.dma_start(out=word_table[z][:].bitcast(I32), in_=x_words[z].bitcast(I32))
 
-        def load_w1(z):
-            rows = w1[z * P * PACK : (z + 1) * P * PACK, :]
-            nc.sync.dma_start(out=w1_raw[z][:], in_=rows.rearrange("(p j) n -> p j n", j=PACK))
+        def load_rows(raw, rows, j0, j1):
+            nc.sync.dma_start(out=raw[:], in_=rows.rearrange("(p j) n -> p j n", j=PACK)[:, j0:j1, :])
 
-        def load_wo(b, w):
-            nc.sync.dma_start(out=wo_raw[b][:], in_=w.rearrange("(p j) n -> p j n", j=PACK))
-
-        def load_w2(h):
-            nc.sync.dma_start(out=w2_raw[h][:], in_=w2.rearrange("(p j) n -> p j n", j=PACK)[:, 2 * h : 2 * h + 2, :])
-
-        def round_w2(engine_copy, h):
-            dst = wo_bf[0][:, :, 2 * h : 2 * h + 2].rearrange("p (c i) j -> p c j i", i=4)
-            src = w2_raw[h][:].rearrange("p j (c i) -> p c j i", i=4)
-            engine_copy(dst, src)
-
-        def load_w1_late(h):
-            rows = w1[P * PACK :, :].rearrange("(p j) n -> p j n", j=PACK)
-            nc.sync.dma_start(out=w1_late[h][:], in_=rows[:, 2 * h : 2 * h + 2, :])
-
-        def round_late_pair(engine_copy, h, u, m0, m1):
-            dst = w1_bf[1][u][:, :, m0:m1, 2 * h : 2 * h + 2].rearrange("p t m j -> p m j t")
-            src = w1_late[h][:].rearrange("p j (m t) -> p m j t", t=PACK)
-            engine_copy(dst, src[:, m0:m1, :, 2 * u : 2 * u + 2])
-
-        def round_w1(engine_copy, z, u, m0, m1):
-            dst = w1_bf[z][u][:, :, m0:m1, :].rearrange("p t m j -> p m j t")
-            src = w1_raw[z][:, :, PACK * m0 : PACK * m1].rearrange("p j (m t) -> p m j t", t=PACK)
+        def round_w1(engine_copy, raw, z, j0, j1, u, m0, m1):
+            dst = w1_bf[z][u][:, :, m0:m1, j0:j1].rearrange("p t m j -> p m j t")
+            src = raw[:, :, PACK * m0 : PACK * m1].rearrange("p j (m t) -> p m j t", t=PACK)
             engine_copy(dst, src[:, :, :, 2 * u : 2 * u + 2])
 
-        def quantise_w1(z, u):
+        def quantise_w1(z, u, i0, i1):
+            cols = slice(i0 * P, i1 * P)
             nc.vector.quantize_mx(
-                out=w1_codes[z][u][:].bitcast(FP8X4),
-                scales=w1_scales[z][u][:],
-                in_=w1_bf[z][u][:].rearrange("p t m j -> p (t m j)"),
+                out=w1_codes[z][u][:, cols].bitcast(FP8X4),
+                scales=w1_scales[z][u][:, cols],
+                in_=w1_bf[z][u][:, i0:i1, :, :].rearrange("p t m j -> p (t m j)"),
             )
 
-        def round_wo(engine_copy, b, n0, n1):
-            dst = wo_bf[b][:, n0:n1, :].rearrange("p (c i) j -> p c j i", i=4)
-            src = wo_raw[b][:, :, n0:n1].rearrange("p j (c i) -> p c j i", i=4)
+        def round_wo(engine_copy, rounded, raw):
+            dst = rounded.rearrange("p (c i) j -> p c j i", i=LINE)
+            src = raw.rearrange("p j (c i) -> p c j i", i=LINE)
             engine_copy(dst, src)
 
-        def quantise_wo(b):
+        def quantise_wo(b, rounded):
             nc.vector.quantize_mx(
-                out=wo_codes[b][:].bitcast(FP8X4), scales=wo_scales[b][:], in_=wo_bf[b][:].rearrange("p n j -> p (n j)")
+                out=wo_codes[b][:].bitcast(FP8X4), scales=wo_scales[b][:], in_=rounded[:].rearrange("p n j -> p (n j)")
             )
 
         def warm_up(z):
@@ -129,11 +111,11 @@ def tile_picked_haar_gelu_p_kernel(tc, x_words, x_scales, w1, w2, w3, offs, out)
                 stop=True,
             )
 
-        def first_product(z, s, d, t, start, stop):
+        def first_product(bank_range, z, s, d, t, start, stop):
             cols = slice((t % 2) * P, (t % 2 + 1) * P)
             entries = slice(d * V + s * HALF, d * V + (s + 1) * HALF)
             nc.tensor.matmul_mx(
-                out=(pre[0][t // 2][:, 2 * d + t % 2, :] if s == 0 else pre[s][d][:, t, :]),
+                out=bank_range,
                 lhsT=w1_codes[z][t // 2][:, cols].bitcast(FP8X4),
                 lhsT_scale=w1_scales[z][t // 2][:, cols],
                 rhs=picked_words[z][:, entries].bitcast(FP4X4),
@@ -142,14 +124,21 @@ def tile_picked_haar_gelu_p_kernel(tc, x_words, x_scales, w1, w2, w3, offs, out)
                 stop=stop,
             )
 
-        def gelu(s, d, v0, v1):
-            nc.scalar.activation(out=hidden[s][d][:, v0:v1, :], in_=pre[s][d][:, :, v0:v1].rearrange("p t v -> p v t"), func=GELU)
+        def product_first_half(z, d, t, start, stop):
+            first_product(pre_first[t // 2][:, 2 * d + t % 2, :], z, 0, d, t, start, stop)
 
-        def gelu_first(u, v0, v1):
-            src = pre[0][u][:, :, v0:v1].rearrange("p (d t) v -> p d v t", d=2)
+        def product_second_half(z, d, t, start, stop):
+            first_product(pre_second[d][:, t, :], z, 1, d, t, start, stop)
+
+        def gelu_first_half(u, v0, v1):
+            src = pre_first[u][:, :, v0:v1].rearrange("p (d t) v -> p d v t", d=2)
             nc.scalar.activation(out=hidden_first[:, u, :, v0:v1, :], in_=src, func=GELU)
 
-        def band_first(b, v0, v1):
+        def gelu_second_half(d, v0, v1):
+            src = pre_second[d][:, :, v0:v1].rearrange("p t v -> p v t")
+            nc.scalar.activation(out=hidden_second[d][:, v0:v1, :], in_=src, func=GELU)
+
+        def band_first_half(b, v0, v1):
             nc.vector.tensor_tensor(
                 out=band_bf[0][:, b, v0:v1, :].rearrange("p v (u t) -> p v u t", u=2),
                 in0=hidden_first[:, :, 0, v0:v1, :].rearrange("p u v t -> p v u t"),
@@ -157,11 +146,11 @@ def tile_picked_haar_gelu_p_kernel(tc, x_words, x_scales, w1, w2, w3, offs, out)
                 op=(ADD if b == 0 else SUB),
             )
 
-        def band(s, b, v0, v1):
+        def band_second_half(b, v0, v1):
             nc.vector.tensor_tensor(
-                out=band_bf[s][:, b, v0:v1, :],
-                in0=hidden[s][0][:, v0:v1, :],
-                in1=hidden[s][1][:, v0:v1, :],
+                out=band_bf[1][:, b, v0:v1, :],
+                in0=hidden_second[0][:, v0:v1, :],
+                in1=hidden_second[1][:, v0:v1, :],
                 op=(ADD if b == 0 else SUB),
             )
 
@@ -203,79 +192,73 @@ def tile_picked_haar_gelu_p_kernel(tc, x_words, x_scales, w1, w2, w3, offs, out)
         for r in range(QUADRANT_ROWS):
             nc.sync.dma_start(out=scale_table[r:P:SHIFT, :].bitcast(I32), in_=scale_rows[r].bitcast(I32))
         nc.scalar.activation(out=preload_out[:], in_=zero_bf[:, 0:8], func=GELU)
-        load_w1(0)
+        load_rows(pass0_raw, w1[: P * PACK, :], 0, PACK)
         for h in range(2):
-            load_w1_late(h)
-        wo_raw.append(None)
+            load_rows(pass1_raw[h], w1[P * PACK :, :], 2 * h, 2 * h + 2)
         w2_raw = [tile([P, 2, N], F32, "w2_raw0")]
-        load_w2(0)
+        load_rows(w2_raw[0], w2, 0, 2)
 
         for z in range(PASSES):
             nc.vector.tensor_copy(picked_words[z][:], word_table[z][:].indirect(offsets[:]))
         nc.vector.tensor_copy(picked_scales[0][:], scale_table[:].indirect(offsets[:]))
-        for p0, p1 in ((0, P - SHIFT),):
-            nc.sync.dma_start(
-                out=picked_scales[1][p0:p1, :].bitcast(I32), in_=picked_scales[0][p0 + SHIFT : p1 + SHIFT, :].bitcast(I32)
-            )
+        nc.sync.dma_start(out=picked_scales[1][0 : P - SHIFT, :].bitcast(I32), in_=picked_scales[0][SHIFT:P, :].bitcast(I32))
         for z in range(PASSES):
             warm_up(z)
         acc[1].append(ps.tile([P, HALF], F32, name="acc11", tag="warm_bank"))
         w2_raw.append(tile_after([P, 2, N], F32, "w2_raw1", "scale_table"))
-        load_w2(1)
-        wo_raw.append(tile_after([P, PACK, N], F32, "wo_raw1", "w1_raw0"))
-        load_wo(1, w3)
+        load_rows(w2_raw[1], w2, 2, PACK)
+        w3_raw = tile_after([P, PACK, N], F32, "w3_raw", "pass0_raw")
+        load_rows(w3_raw, w3, 0, PACK)
 
-        round_w1(nc.scalar.copy, 0, 0, 0, P)
-        round_w1(nc.vector.tensor_copy, 0, 1, 0, VECTOR_SHARE[0])
-        round_w1(nc.scalar.copy, 0, 1, VECTOR_SHARE[0], P)
+        round_w1(nc.scalar.copy, pass0_raw, 0, 0, PACK, 0, 0, P)
+        round_w1(nc.vector.tensor_copy, pass0_raw, 0, 0, PACK, 1, 0, VECTOR_SHARE_PASS0)
+        round_w1(nc.scalar.copy, pass0_raw, 0, 0, PACK, 1, VECTOR_SHARE_PASS0, P)
         for u in range(2):
-            quantise_w1(0, u)
+            quantise_w1(0, u, 0, 2)
         for t in range(PACK):
             for d in range(2):
-                first_product(0, 0, d, t, t % 2 == 0 and d == 0, False)
+                product_first_half(0, d, t, t % 2 == 0 and d == 0, False)
 
-        round_late_pair(nc.vector.tensor_copy, 0, 0, 0, P)
-        round_late_pair(nc.scalar.copy, 0, 1, 0, P)
-        round_late_pair(nc.vector.tensor_copy, 1, 0, 0, P)
-        round_late_pair(nc.scalar.copy, 1, 1, 40, P)
-        round_late_pair(nc.vector.tensor_copy, 1, 1, 0, 40)
-        for u in range(2):
-            quantise_w1(1, u)
-        for u in range(2):
+        round_w1(nc.vector.tensor_copy, pass1_raw[0], 1, 0, 2, 0, 0, P)
+        round_w1(nc.scalar.copy, pass1_raw[0], 1, 0, 2, 1, 0, P)
+        round_w1(nc.vector.tensor_copy, pass1_raw[1], 1, 2, PACK, 0, 0, P)
+        round_w1(nc.scalar.copy, pass1_raw[1], 1, 2, PACK, 1, VECTOR_SHARE_LAST, P)
+        round_w1(nc.vector.tensor_copy, pass1_raw[1], 1, 2, PACK, 1, 0, VECTOR_SHARE_LAST)
+        for i in range(2):
+            quantise_w1(1, 0, i, i + 1)
+        quantise_w1(1, 1, 0, 2)
+        for t in range(PACK):
             for d in range(2):
-                for t in (2 * u, 2 * u + 1):
-                    first_product(1, 0, d, t, False, d == 1 and t % 2 == 1)
+                product_first_half(1, d, t, False, t % 2 == 1 and d == 1)
         for d in range(2):
             for z in reversed(range(PASSES)):
                 for t in reversed(range(PACK)):
-                    first_product(z, 1, d, t, z == PASSES - 1 and t == PACK - 1, z == 0 and t == 0)
+                    product_second_half(z, d, t, z == PASSES - 1 and t == PACK - 1, z == 0 and t == 0)
 
-        round_w2(nc.scalar.copy, 0)
-        gelu_first(0, 0, HALF)
-        for v0, v1 in ((0, 32), (32, HALF)):
-            gelu_first(1, v0, v1)
-        gelu(1, 0, 0, HALF)
-        for v0, v1 in ((0, 96), (96, HALF)):
-            gelu(1, 1, v0, v1)
+        round_wo(nc.scalar.copy, w2_bf[:, :, 0:2], w2_raw[0][:])
+        gelu_first_half(0, 0, HALF)
+        for v0, v1 in FIRST_PIECES:
+            gelu_first_half(1, v0, v1)
+        gelu_second_half(0, 0, HALF)
+        for v0, v1 in SECOND_PIECES:
+            gelu_second_half(1, v0, v1)
 
-        round_w2(nc.vector.tensor_copy, 1)
-        wo_bf.append(tile_after([P, N, PACK], BF16, "wo_bf1", "w1_codes00"))
-        round_wo(nc.vector.tensor_copy, 1, 0, 16)
-        round_wo(nc.scalar.copy, 1, 16, N)
-        quantise_wo(0)
+        round_wo(nc.vector.tensor_copy, w2_bf[:, :, 2:PACK], w2_raw[1][:])
+        w3_bf = tile_after([P, N, PACK], BF16, "w3_bf", "w1_codes00")
+        round_wo(nc.scalar.copy, w3_bf[:], w3_raw[:])
+        quantise_wo(0, w2_bf)
 
-        band_bf.append(tile([P, 2, HALF, PACK], BF16, "band_bf0"))
-        band_bf.append(tile([P, 2, HALF, PACK], BF16, "band_bf1"))
-        for v0, v1 in ((0, 32), (32, HALF)):
+        band_bf = [tile([P, 2, HALF, PACK], BF16, "band_bf%d" % s) for s in range(2)]
+        for v0, v1 in FIRST_PIECES:
             for b in range(2):
-                band_first(b, v0, v1)
+                band_first_half(b, v0, v1)
         for b in range(2):
             quantise_band(0, b)
-        for v0, v1 in ((0, 96), (96, HALF)):
+        for v0, v1 in SECOND_PIECES:
             for b in range(2):
-                band(1, b, v0, v1)
+                band_second_half(b, v0, v1)
         quantise_band(1, 0)
-        quantise_wo(1)
+        quantise_wo(1, w3_bf)
         quantise_band(1, 1)
 
         for b in range(2):

@@ -26,7 +26,7 @@ HALF = V // 2
 QUADRANT_ROWS = 4
 SHIFT = 16
 LINE = 4
-VECTOR_SHARE_PASS0 = 88
+VECTOR_SHARE_PASS0 = (72, 16)
 VECTOR_SHARE_LAST = 40
 FIRST_PIECES = ((0, 32), (32, 64), (64, HALF))
 SECOND_PIECES = ((0, 96), (96, HALF))
@@ -61,15 +61,12 @@ def tile_picked_haar_gelu_p_kernel(tc, x_words, x_scales, w1, w2, w3, offs, out)
         hidden_second = [tile([P, HALF, PACK], F32, "hidden_second%d" % d) for d in range(2)]
         band_codes = [[tile([P, HALF], U32, "band_codes%d%d" % (s, b)) for b in range(2)] for s in range(2)]
         band_scales = [[tile([P, HALF], U8, "band_scales%d%d" % (s, b)) for b in range(2)] for s in range(2)]
-        result = [tile([P, 2, HALF], F32, "result%d" % s) for s in range(2)]
+        result = [tile([P, 2, HALF], F32, "result%d" % mb) for mb in range(2)]
         preload_out = tile([P, 8], F32, "preload_out")
         pre_first = [ps.tile([P, PACK, HALF], F32, name="pre_first%d" % u) for u in range(2)]
         pre_second = [ps.tile([P, PACK, HALF], F32, name="pre_second%d" % d) for d in range(2)]
-        warm_bank = ps.tile([P, S], F32, name="warm_bank")
-        acc = [[ps.tile([P, HALF], F32, name="acc0%d" % mb) for mb in range(2)], [ps.tile([P, HALF], F32, name="acc10")]]
-        zero_bf = tile([P, P * PACK], BF16, "zero_bf")
-        zero_codes = tile([P, P], U32, "zero_codes")
-        zero_scales = tile([P, P], U8, "zero_scales")
+        acc = [[ps.tile([P, HALF], F32, name="acc%d%d" % (s, mb)) for mb in range(2)] for s in range(2)]
+        preload_in = tile([P, 8], F32, "preload_in")
 
         def load_words(z):
             nc.sync.dma_start(out=word_table[z][:].bitcast(I32), in_=x_words[z].bitcast(I32))
@@ -77,17 +74,16 @@ def tile_picked_haar_gelu_p_kernel(tc, x_words, x_scales, w1, w2, w3, offs, out)
         def load_rows(raw, rows, j0, j1):
             nc.sync.dma_start(out=raw[:], in_=rows.rearrange("(p j) n -> p j n", j=PACK)[:, j0:j1, :])
 
-        def round_w1(engine_copy, raw, z, j0, j1, u, m0, m1):
+        def round_w1(engine_copy, raw, z, j0, j1, u, m0, m1, first_m=0):
             dst = w1_bf[z][u][:, :, m0:m1, j0:j1].rearrange("p t m j -> p m j t")
-            src = raw[:, :, PACK * m0 : PACK * m1].rearrange("p j (m t) -> p m j t", t=PACK)
+            src = raw[:, :, PACK * (m0 - first_m) : PACK * (m1 - first_m)].rearrange("p j (m t) -> p m j t", t=PACK)
             engine_copy(dst, src[:, :, :, 2 * u : 2 * u + 2])
 
-        def quantise_w1(z, u, i0, i1):
-            cols = slice(i0 * P, i1 * P)
+        def quantise_w1(z, u, c0, c1):
             nc.vector.quantize_mx(
-                out=w1_codes[z][u][:, cols].bitcast(FP8X4),
-                scales=w1_scales[z][u][:, cols],
-                in_=w1_bf[z][u][:, i0:i1, :, :].rearrange("p t m j -> p (t m j)"),
+                out=w1_codes[z][u][:, c0:c1].bitcast(FP8X4),
+                scales=w1_scales[z][u][:, c0:c1],
+                in_=w1_bf[z][u][:].rearrange("p t m j -> p (t m j)")[:, PACK * c0 : PACK * c1],
             )
 
         def round_wo(engine_copy, rounded, raw):
@@ -95,20 +91,11 @@ def tile_picked_haar_gelu_p_kernel(tc, x_words, x_scales, w1, w2, w3, offs, out)
             src = raw.rearrange("p j (c i) -> p c j i", i=LINE)
             engine_copy(dst, src)
 
-        def quantise_wo(b, rounded):
+        def quantise_wo(b, rounded, n0, n1):
             nc.vector.quantize_mx(
-                out=wo_codes[b][:].bitcast(FP8X4), scales=wo_scales[b][:], in_=rounded[:].rearrange("p n j -> p (n j)")
-            )
-
-        def warm_up(z):
-            nc.tensor.matmul_mx(
-                out=warm_bank[:],
-                lhsT=zero_codes[:].bitcast(FP8X4),
-                lhsT_scale=zero_scales[:],
-                rhs=picked_words[z][:].bitcast(FP4X4),
-                rhs_scale=picked_scales[0][:],
-                start=True,
-                stop=True,
+                out=wo_codes[b][:, n0:n1].bitcast(FP8X4),
+                scales=wo_scales[b][:, n0:n1],
+                in_=rounded[:, n0:n1, :].rearrange("p n j -> p (n j)"),
             )
 
         def first_product(bank_range, z, s, d, t, start, stop):
@@ -161,29 +148,30 @@ def tile_picked_haar_gelu_p_kernel(tc, x_words, x_scales, w1, w2, w3, offs, out)
                 in_=band_bf[s][:, b, :, :].rearrange("p v t -> p (v t)"),
             )
 
-        def second_product(s, b):
-            for mb in range(2):
-                cols = slice(mb * P, (mb + 1) * P)
-                nc.tensor.matmul_mx(
-                    out=acc[s][mb][:],
-                    lhsT=wo_codes[b][:, cols].bitcast(FP8X4),
-                    lhsT_scale=wo_scales[b][:, cols],
-                    rhs=band_codes[s][b][:].bitcast(FP8X4),
-                    rhs_scale=band_scales[s][b][:],
-                    start=(b == 0),
-                    stop=(b == 1),
-                )
+        def second_product(s, b, mb):
+            cols = slice(mb * P, (mb + 1) * P)
+            nc.tensor.matmul_mx(
+                out=acc[s][mb][:],
+                lhsT=wo_codes[b][:, cols].bitcast(FP8X4),
+                lhsT_scale=wo_scales[b][:, cols],
+                rhs=band_codes[s][b][:].bitcast(FP8X4),
+                rhs_scale=band_scales[s][b][:],
+                start=(b == 0),
+                stop=(b == 1),
+            )
 
-        def halve_and_store(s):
-            nc.scalar.activation(out=result[s][:, 0, :], in_=acc[s][0][:], func=COPY, scale=0.5)
-            nc.vector.tensor_scalar(out=result[s][:, 1, :], in0=acc[s][1][:], scalar1=0.5, scalar2=None, op0=MULT)
-            dst = out.rearrange("(mb p) v -> p mb v", p=P)[:, :, s * HALF : (s + 1) * HALF]
-            nc.sync.dma_start(out=dst, in_=result[s][:])
+        def halve_on_scalar(s, mb):
+            nc.scalar.activation(out=result[mb][:, s, :], in_=acc[s][mb][:], func=COPY, scale=0.5)
+
+        def halve_on_vector(s, mb):
+            nc.vector.tensor_scalar(out=result[mb][:, s, :], in0=acc[s][mb][:], scalar1=0.5, scalar2=None, op0=MULT)
+
+        def store(mb):
+            nc.sync.dma_start(out=out[mb * P : (mb + 1) * P, :], in_=result[mb][:].rearrange("p s v -> p (s v)"))
 
         nc.gpsimd.memset(scale_table[:].bitcast(I32), 0)
-        nc.vector.memset(zero_bf[:].bitcast(I32), 0)
+        nc.vector.memset(preload_in[:], 0.0)
         nc.vector.memset(picked_scales[1][:].bitcast(I32), 0)
-        nc.vector.quantize_mx(out=zero_codes[:].bitcast(FP8X4), scales=zero_scales[:], in_=zero_bf[:])
 
         load_words(0)
         nc.sync.dma_start(out=offsets[:], in_=offs)
@@ -191,7 +179,7 @@ def tile_picked_haar_gelu_p_kernel(tc, x_words, x_scales, w1, w2, w3, offs, out)
         scale_rows = x_scales.rearrange("z (q r) n -> r q z n", r=QUADRANT_ROWS)
         for r in range(QUADRANT_ROWS):
             nc.sync.dma_start(out=scale_table[r:P:SHIFT, :].bitcast(I32), in_=scale_rows[r].bitcast(I32))
-        nc.scalar.activation(out=preload_out[:], in_=zero_bf[:, 0:8], func=GELU)
+        nc.scalar.activation(out=preload_out[:], in_=preload_in[:], func=GELU)
         load_rows(pass0_raw, w1[: P * PACK, :], 0, PACK)
         for h in range(2):
             load_rows(pass1_raw[h], w1[P * PACK :, :], 2 * h, 2 * h + 2)
@@ -202,22 +190,24 @@ def tile_picked_haar_gelu_p_kernel(tc, x_words, x_scales, w1, w2, w3, offs, out)
             nc.vector.tensor_copy(picked_words[z][:], word_table[z][:].indirect(offsets[:]))
         nc.vector.tensor_copy(picked_scales[0][:], scale_table[:].indirect(offsets[:]))
         nc.sync.dma_start(out=picked_scales[1][0 : P - SHIFT, :].bitcast(I32), in_=picked_scales[0][SHIFT:P, :].bitcast(I32))
-        for z in range(PASSES):
-            warm_up(z)
-        acc[1].append(ps.tile([P, HALF], F32, name="acc11", tag="warm_bank"))
         w2_raw.append(tile_after([P, 2, N], F32, "w2_raw1", "scale_table"))
         load_rows(w2_raw[1], w2, 2, PACK)
         w3_raw = tile_after([P, PACK, N], F32, "w3_raw", "pass0_raw")
         load_rows(w3_raw, w3, 0, PACK)
 
-        round_w1(nc.scalar.copy, pass0_raw, 0, 0, PACK, 0, 0, P)
-        round_w1(nc.vector.tensor_copy, pass0_raw, 0, 0, PACK, 1, 0, VECTOR_SHARE_PASS0)
-        round_w1(nc.scalar.copy, pass0_raw, 0, 0, PACK, 1, VECTOR_SHARE_PASS0, P)
         for u in range(2):
-            quantise_w1(0, u, 0, 2)
-        for t in range(PACK):
+            round_w1(nc.vector.tensor_copy, pass0_raw, 0, 0, PACK, u, 0, VECTOR_SHARE_PASS0[u])
+            round_w1(nc.scalar.copy, pass0_raw, 0, 0, PACK, u, VECTOR_SHARE_PASS0[u], P)
+        for i in range(2):
+            quantise_w1(0, 0, i * P, (i + 1) * P)
+        quantise_w1(0, 1, 0, 2 * P)
+        for t in range(2):
             for d in range(2):
-                product_first_half(0, d, t, t % 2 == 0 and d == 0, False)
+                product_first_half(0, d, t, t == 0 and d == 0, False)
+                product_second_half(0, d, t, t == 0, False)
+        for t in range(2, PACK):
+            for d in range(2):
+                product_first_half(0, d, t, t == 2 and d == 0, False)
 
         round_w1(nc.vector.tensor_copy, pass1_raw[0], 1, 0, 2, 0, 0, P)
         round_w1(nc.scalar.copy, pass1_raw[0], 1, 0, 2, 1, 0, P)
@@ -225,15 +215,16 @@ def tile_picked_haar_gelu_p_kernel(tc, x_words, x_scales, w1, w2, w3, offs, out)
         round_w1(nc.scalar.copy, pass1_raw[1], 1, 2, PACK, 1, VECTOR_SHARE_LAST, P)
         round_w1(nc.vector.tensor_copy, pass1_raw[1], 1, 2, PACK, 1, 0, VECTOR_SHARE_LAST)
         for i in range(2):
-            quantise_w1(1, 0, i, i + 1)
-        quantise_w1(1, 1, 0, 2)
+            quantise_w1(1, 0, i * P, (i + 1) * P)
+        quantise_w1(1, 1, 0, 2 * P)
         for t in range(PACK):
             for d in range(2):
                 product_first_half(1, d, t, False, t % 2 == 1 and d == 1)
         for d in range(2):
-            for z in reversed(range(PASSES)):
-                for t in reversed(range(PACK)):
-                    product_second_half(z, d, t, z == PASSES - 1 and t == PACK - 1, z == 0 and t == 0)
+            for t in reversed(range(PACK)):
+                product_second_half(1, d, t, False, False)
+            for t in reversed(range(2, PACK)):
+                product_second_half(0, d, t, False, t == 2)
 
         round_wo(nc.scalar.copy, w2_bf[:, :, 0:2], w2_raw[0][:])
         gelu_first_half(0, 0, HALF)
@@ -244,9 +235,10 @@ def tile_picked_haar_gelu_p_kernel(tc, x_words, x_scales, w1, w2, w3, offs, out)
             gelu_second_half(1, v0, v1)
 
         round_wo(nc.vector.tensor_copy, w2_bf[:, :, 2:PACK], w2_raw[1][:])
-        w3_bf = tile_after([P, N, PACK], BF16, "w3_bf", "w1_codes00")
-        round_wo(nc.scalar.copy, w3_bf[:], w3_raw[:])
-        quantise_wo(0, w2_bf)
+        w3_bf = tile_after([P, N, PACK], BF16, "w3_bf", "w1_codes01")
+        for mb in range(2):
+            round_wo(nc.scalar.copy, w3_bf[:, mb * P : (mb + 1) * P, :], w3_raw[:, :, mb * P : (mb + 1) * P])
+        quantise_wo(0, w2_bf, 0, N)
 
         band_bf = [tile([P, 2, HALF, PACK], BF16, "band_bf%d" % s) for s in range(2)]
         for v0, v1 in FIRST_PIECES:
@@ -257,12 +249,20 @@ def tile_picked_haar_gelu_p_kernel(tc, x_words, x_scales, w1, w2, w3, offs, out)
         for v0, v1 in SECOND_PIECES:
             for b in range(2):
                 band_second_half(b, v0, v1)
-        quantise_band(1, 0)
-        quantise_wo(1, w3_bf)
-        quantise_band(1, 1)
-
+        quantise_wo(1, w3_bf, 0, P)
         for b in range(2):
-            for s in range(2):
-                second_product(s, b)
+            quantise_band(1, b)
+        quantise_wo(1, w3_bf, P, N)
+
         for s in range(2):
-            halve_and_store(s)
+            for mb in range(2):
+                second_product(s, 0, mb)
+        for mb in range(2):
+            for s in range(2):
+                second_product(s, 1, mb)
+        for s in range(2):
+            halve_on_scalar(s, 0)
+        store(0)
+        halve_on_vector(0, 1)
+        halve_on_scalar(1, 1)
+        store(1)

@@ -26,7 +26,7 @@ HALF = V // 2
 QUADRANT_ROWS = 4
 SHIFT = 16
 LINE = 4
-VECTOR_SHARE_PASS0 = (72, 16)
+VECTOR_SHARE_PASS0 = 88
 VECTOR_SHARE_LAST = 40
 FIRST_PIECES = ((0, 32), (32, 64), (64, HALF))
 SECOND_PIECES = ((0, 96), (96, HALF))
@@ -54,29 +54,33 @@ def tile_picked_haar_gelu_p_kernel(tc, x_words, x_scales, w1, w2, w3, offs, out)
         w1_bf = [[tile([P, 2, P, PACK], BF16, "w1_bf%d%d" % (z, u)) for u in range(2)] for z in range(PASSES)]
         w1_codes = [[tile([P, 2 * P], U32, "w1_codes%d%d" % (z, u)) for u in range(2)] for z in range(PASSES)]
         w1_scales = [[tile([P, 2 * P], U8, "w1_scales%d%d" % (z, u)) for u in range(2)] for z in range(PASSES)]
-        w2_bf = tile([P, N, PACK], BF16, "w2_bf")
+        w2_bf = tile([P, 2, P, PACK], BF16, "w2_bf")
         wo_codes = [tile([P, N], U32, "wo_codes%d" % b) for b in range(2)]
         wo_scales = [tile([P, N], U8, "wo_scales%d" % b) for b in range(2)]
         hidden_first = tile([P, 2, 2, HALF, 2], F32, "hidden_first")
         hidden_second = [tile([P, HALF, PACK], F32, "hidden_second%d" % d) for d in range(2)]
         band_codes = [[tile([P, HALF], U32, "band_codes%d%d" % (s, b)) for b in range(2)] for s in range(2)]
         band_scales = [[tile([P, HALF], U8, "band_scales%d%d" % (s, b)) for b in range(2)] for s in range(2)]
-        result = [tile([P, 2, HALF], F32, "result%d" % mb) for mb in range(2)]
+        result = tile([P, 2, 2, HALF], F32, "result")
         preload_out = tile([P, 8], F32, "preload_out")
         pre_first = [ps.tile([P, PACK, HALF], F32, name="pre_first%d" % u) for u in range(2)]
         pre_second = [ps.tile([P, PACK, HALF], F32, name="pre_second%d" % d) for d in range(2)]
-        acc = [[ps.tile([P, HALF], F32, name="acc%d%d" % (s, mb)) for mb in range(2)] for s in range(2)]
+        warm_bank = ps.tile([P, S], F32, name="warm_bank")
+        acc = [[ps.tile([P, HALF], F32, name="acc0%d" % mb) for mb in range(2)], [ps.tile([P, HALF], F32, name="acc10")]]
+        warm_bf = tile([P, H], BF16, "warm_bf")
+        warm_codes = tile([P, P], U32, "warm_codes")
+        warm_scales = tile([P, P], U8, "warm_scales")
         preload_in = tile([P, 8], F32, "preload_in")
 
         def load_words(z):
             nc.sync.dma_start(out=word_table[z][:].bitcast(I32), in_=x_words[z].bitcast(I32))
 
         def load_rows(raw, rows, j0, j1):
-            nc.sync.dma_start(out=raw[:], in_=rows.rearrange("(p j) n -> p j n", j=PACK)[:, j0:j1, :])
+            nc.sync.dma_start(out=raw, in_=rows.rearrange("(p j) n -> p j n", j=PACK)[:, j0:j1, :])
 
-        def round_w1(engine_copy, raw, z, j0, j1, u, m0, m1, first_m=0):
+        def round_w1(engine_copy, raw, z, j0, j1, u, m0, m1, first_j=0):
             dst = w1_bf[z][u][:, :, m0:m1, j0:j1].rearrange("p t m j -> p m j t")
-            src = raw[:, :, PACK * (m0 - first_m) : PACK * (m1 - first_m)].rearrange("p j (m t) -> p m j t", t=PACK)
+            src = raw[:, j0 - first_j : j1 - first_j, PACK * m0 : PACK * m1].rearrange("p j (m t) -> p m j t", t=PACK)
             engine_copy(dst, src[:, :, :, 2 * u : 2 * u + 2])
 
         def quantise_w1(z, u, c0, c1):
@@ -86,16 +90,32 @@ def tile_picked_haar_gelu_p_kernel(tc, x_words, x_scales, w1, w2, w3, offs, out)
                 in_=w1_bf[z][u][:].rearrange("p t m j -> p (t m j)")[:, PACK * c0 : PACK * c1],
             )
 
-        def round_wo(engine_copy, rounded, raw):
-            dst = rounded.rearrange("p (c i) j -> p c j i", i=LINE)
-            src = raw.rearrange("p j (c i) -> p c j i", i=LINE)
+        def round_w2(engine_copy, h):
+            dst = w2_bf[:, :, :, 2 * h : 2 * h + 2].rearrange("p mb (c i) j -> p c j i mb", i=2)
+            src = w2_raw[h][:].rearrange("p j (c i mb) -> p c j i mb", i=2, mb=2)
             engine_copy(dst, src)
+
+        def round_w3(mb):
+            dst = w3_bf[:, mb].rearrange("p (c i) j -> p c j i", i=2)
+            src = w3_raw[:].rearrange("p j (c i mb) -> p mb c j i", i=2, mb=2)[:, mb]
+            nc.scalar.copy(dst, src)
 
         def quantise_wo(b, rounded, n0, n1):
             nc.vector.quantize_mx(
                 out=wo_codes[b][:, n0:n1].bitcast(FP8X4),
                 scales=wo_scales[b][:, n0:n1],
-                in_=rounded[:, n0:n1, :].rearrange("p n j -> p (n j)"),
+                in_=rounded[:].rearrange("p mb m j -> p (mb m j)")[:, PACK * n0 : PACK * n1],
+            )
+
+        def warm_up(z):
+            nc.tensor.matmul_mx(
+                out=warm_bank[:],
+                lhsT=warm_codes[:].bitcast(FP8X4),
+                lhsT_scale=warm_scales[:],
+                rhs=picked_words[z][:].bitcast(FP4X4),
+                rhs_scale=picked_scales[0][:],
+                start=True,
+                stop=True,
             )
 
         def first_product(bank_range, z, s, d, t, start, stop):
@@ -161,13 +181,10 @@ def tile_picked_haar_gelu_p_kernel(tc, x_words, x_scales, w1, w2, w3, offs, out)
             )
 
         def halve_on_scalar(s, mb):
-            nc.scalar.activation(out=result[mb][:, s, :], in_=acc[s][mb][:], func=COPY, scale=0.5)
+            nc.scalar.activation(out=result[:, mb, s, :], in_=acc[s][mb][:], func=COPY, scale=0.5)
 
         def halve_on_vector(s, mb):
-            nc.vector.tensor_scalar(out=result[mb][:, s, :], in0=acc[s][mb][:], scalar1=0.5, scalar2=None, op0=MULT)
-
-        def store(mb):
-            nc.sync.dma_start(out=out[mb * P : (mb + 1) * P, :], in_=result[mb][:].rearrange("p s v -> p (s v)"))
+            nc.vector.tensor_scalar(out=result[:, mb, s, :], in0=acc[s][mb][:], scalar1=0.5, scalar2=None, op0=MULT)
 
         nc.gpsimd.memset(scale_table[:].bitcast(I32), 0)
         nc.vector.memset(preload_in[:], 0.0)
@@ -180,40 +197,42 @@ def tile_picked_haar_gelu_p_kernel(tc, x_words, x_scales, w1, w2, w3, offs, out)
         for r in range(QUADRANT_ROWS):
             nc.sync.dma_start(out=scale_table[r:P:SHIFT, :].bitcast(I32), in_=scale_rows[r].bitcast(I32))
         nc.scalar.activation(out=preload_out[:], in_=preload_in[:], func=GELU)
-        load_rows(pass0_raw, w1[: P * PACK, :], 0, PACK)
         for h in range(2):
-            load_rows(pass1_raw[h], w1[P * PACK :, :], 2 * h, 2 * h + 2)
+            load_rows(pass0_raw[:, 2 * h : 2 * h + 2, :], w1[: P * PACK, :], 2 * h, 2 * h + 2)
+        for h in range(2):
+            load_rows(pass1_raw[h][:], w1[P * PACK :, :], 2 * h, 2 * h + 2)
         w2_raw = [tile([P, 2, N], F32, "w2_raw0")]
-        load_rows(w2_raw[0], w2, 0, 2)
+        load_rows(w2_raw[0][:], w2, 0, 2)
 
         for z in range(PASSES):
             nc.vector.tensor_copy(picked_words[z][:], word_table[z][:].indirect(offsets[:]))
         nc.vector.tensor_copy(picked_scales[0][:], scale_table[:].indirect(offsets[:]))
         nc.sync.dma_start(out=picked_scales[1][0 : P - SHIFT, :].bitcast(I32), in_=picked_scales[0][SHIFT:P, :].bitcast(I32))
         w2_raw.append(tile_after([P, 2, N], F32, "w2_raw1", "scale_table"))
-        load_rows(w2_raw[1], w2, 2, PACK)
+        load_rows(w2_raw[1][:], w2, 2, PACK)
         w3_raw = tile_after([P, PACK, N], F32, "w3_raw", "pass0_raw")
-        load_rows(w3_raw, w3, 0, PACK)
+        load_rows(w3_raw[:], w3, 0, PACK)
 
+        nc.scalar.copy(warm_bf[:], pass0_raw[:, 0, :])
+        nc.vector.quantize_mx(out=warm_codes[:].bitcast(FP8X4), scales=warm_scales[:], in_=warm_bf[:])
+        for z in range(PASSES):
+            warm_up(z)
+        acc[1].append(ps.tile([P, HALF], F32, name="acc11", tag="warm_bank"))
+
+        round_w1(nc.scalar.copy, pass0_raw, 0, 0, PACK, 0, 0, P)
+        round_w1(nc.vector.tensor_copy, pass0_raw, 0, 0, PACK, 1, 0, VECTOR_SHARE_PASS0)
+        round_w1(nc.scalar.copy, pass0_raw, 0, 0, PACK, 1, VECTOR_SHARE_PASS0, P)
         for u in range(2):
-            round_w1(nc.vector.tensor_copy, pass0_raw, 0, 0, PACK, u, 0, VECTOR_SHARE_PASS0[u])
-            round_w1(nc.scalar.copy, pass0_raw, 0, 0, PACK, u, VECTOR_SHARE_PASS0[u], P)
-        for i in range(2):
-            quantise_w1(0, 0, i * P, (i + 1) * P)
-        quantise_w1(0, 1, 0, 2 * P)
-        for t in range(2):
+            quantise_w1(0, u, 0, 2 * P)
+        for t in range(PACK):
             for d in range(2):
-                product_first_half(0, d, t, t == 0 and d == 0, False)
-                product_second_half(0, d, t, t == 0, False)
-        for t in range(2, PACK):
-            for d in range(2):
-                product_first_half(0, d, t, t == 2 and d == 0, False)
+                product_first_half(0, d, t, t % 2 == 0 and d == 0, False)
 
         round_w1(nc.vector.tensor_copy, pass1_raw[0], 1, 0, 2, 0, 0, P)
         round_w1(nc.scalar.copy, pass1_raw[0], 1, 0, 2, 1, 0, P)
-        round_w1(nc.vector.tensor_copy, pass1_raw[1], 1, 2, PACK, 0, 0, P)
-        round_w1(nc.scalar.copy, pass1_raw[1], 1, 2, PACK, 1, VECTOR_SHARE_LAST, P)
-        round_w1(nc.vector.tensor_copy, pass1_raw[1], 1, 2, PACK, 1, 0, VECTOR_SHARE_LAST)
+        round_w1(nc.vector.tensor_copy, pass1_raw[1], 1, 2, PACK, 0, 0, P, 2)
+        round_w1(nc.scalar.copy, pass1_raw[1], 1, 2, PACK, 1, VECTOR_SHARE_LAST, P, 2)
+        round_w1(nc.vector.tensor_copy, pass1_raw[1], 1, 2, PACK, 1, 0, VECTOR_SHARE_LAST, 2)
         for i in range(2):
             quantise_w1(1, 0, i * P, (i + 1) * P)
         quantise_w1(1, 1, 0, 2 * P)
@@ -221,12 +240,11 @@ def tile_picked_haar_gelu_p_kernel(tc, x_words, x_scales, w1, w2, w3, offs, out)
             for d in range(2):
                 product_first_half(1, d, t, False, t % 2 == 1 and d == 1)
         for d in range(2):
-            for t in reversed(range(PACK)):
-                product_second_half(1, d, t, False, False)
-            for t in reversed(range(2, PACK)):
-                product_second_half(0, d, t, False, t == 2)
+            for z in reversed(range(PASSES)):
+                for t in reversed(range(PACK)):
+                    product_second_half(z, d, t, z == PASSES - 1 and t == PACK - 1, z == 0 and t == 0)
 
-        round_wo(nc.scalar.copy, w2_bf[:, :, 0:2], w2_raw[0][:])
+        round_w2(nc.scalar.copy, 0)
         gelu_first_half(0, 0, HALF)
         for v0, v1 in FIRST_PIECES:
             gelu_first_half(1, v0, v1)
@@ -234,10 +252,10 @@ def tile_picked_haar_gelu_p_kernel(tc, x_words, x_scales, w1, w2, w3, offs, out)
         for v0, v1 in SECOND_PIECES:
             gelu_second_half(1, v0, v1)
 
-        round_wo(nc.vector.tensor_copy, w2_bf[:, :, 2:PACK], w2_raw[1][:])
-        w3_bf = tile_after([P, N, PACK], BF16, "w3_bf", "w1_codes01")
+        round_w2(nc.vector.tensor_copy, 1)
+        w3_bf = tile_after([P, 2, P, PACK], BF16, "w3_bf", "w1_codes00")
         for mb in range(2):
-            round_wo(nc.scalar.copy, w3_bf[:, mb * P : (mb + 1) * P, :], w3_raw[:, :, mb * P : (mb + 1) * P])
+            round_w3(mb)
         quantise_wo(0, w2_bf, 0, N)
 
         band_bf = [tile([P, 2, HALF, PACK], BF16, "band_bf%d" % s) for s in range(2)]
@@ -262,7 +280,6 @@ def tile_picked_haar_gelu_p_kernel(tc, x_words, x_scales, w1, w2, w3, offs, out)
                 second_product(s, 1, mb)
         for s in range(2):
             halve_on_scalar(s, 0)
-        store(0)
         halve_on_vector(0, 1)
         halve_on_scalar(1, 1)
-        store(1)
+        nc.sync.dma_start(out=out.rearrange("(p mb) v -> p (mb v)", mb=2), in_=result[:].rearrange("p mb s v -> p (mb s v)"))

@@ -107,12 +107,12 @@ def tile_picked_haar_gelu_p_kernel(tc, x_words, x_scales, w1, w2, w3, offs, out)
                 in_=rounded[:].rearrange("p mb m j -> p (mb m j)")[:, PACK * n0 : PACK * n1],
             )
 
-        def warm_up(z):
+        def warm_up():
             nc.tensor.matmul_mx(
                 out=warm_bank[:],
                 lhsT=warm_codes[:].bitcast(FP8X4),
                 lhsT_scale=warm_scales[:],
-                rhs=picked_words[z][:].bitcast(FP4X4),
+                rhs=picked_words[0][:].bitcast(FP4X4),
                 rhs_scale=picked_scales[0][:],
                 start=True,
                 stop=True,
@@ -215,8 +215,7 @@ def tile_picked_haar_gelu_p_kernel(tc, x_words, x_scales, w1, w2, w3, offs, out)
 
         nc.scalar.copy(warm_bf[:], pass0_raw[:, 0, :])
         nc.vector.quantize_mx(out=warm_codes[:].bitcast(FP8X4), scales=warm_scales[:], in_=warm_bf[:])
-        for z in range(PASSES):
-            warm_up(z)
+        warm_up()
         acc[1].append(ps.tile([P, HALF], F32, name="acc11", tag="warm_bank"))
 
         round_w1(nc.scalar.copy, pass0_raw, 0, 0, PACK, 0, 0, P)

@@ -54,7 +54,7 @@ def tile_picked_haar_gelu_p_kernel(tc, x_words, x_scales, w1, w2, w3, offs, out)
         w1_bf = [[tile([P, 2, P, PACK], BF16, "w1_bf%d%d" % (z, u)) for u in range(2)] for z in range(PASSES)]
         w1_codes = [[tile([P, 2 * P], U32, "w1_codes%d%d" % (z, u)) for u in range(2)] for z in range(PASSES)]
         w1_scales = [[tile([P, 2 * P], U8, "w1_scales%d%d" % (z, u)) for u in range(2)] for z in range(PASSES)]
-        w2_bf = tile([P, 2, P, PACK], BF16, "w2_bf")
+        w2_bf = tile([P, N, PACK], BF16, "w2_bf")
         wo_codes = [tile([P, N], U32, "wo_codes%d" % b) for b in range(2)]
         wo_scales = [tile([P, N], U8, "wo_scales%d" % b) for b in range(2)]
         hidden_first = tile([P, 2, 2, HALF, 2], F32, "hidden_first")
@@ -90,21 +90,19 @@ def tile_picked_haar_gelu_p_kernel(tc, x_words, x_scales, w1, w2, w3, offs, out)
                 in_=w1_bf[z][u][:].rearrange("p t m j -> p (t m j)")[:, PACK * c0 : PACK * c1],
             )
 
-        def round_w2(engine_copy, h):
-            dst = w2_bf[:, :, :, 2 * h : 2 * h + 2].rearrange("p mb (c i) j -> p c j i mb", i=2)
-            src = w2_raw[h][:].rearrange("p j (c i mb) -> p c j i mb", i=2, mb=2)
-            engine_copy(dst, src)
+        def round_w2(engine_copy, h, n0, n1):
+            dst = w2_bf[:, n0:n1, 2 * h : 2 * h + 2].rearrange("p (c i) j -> p c j i", i=LINE)
+            engine_copy(dst, w2_raw[h][:, :, n0:n1].rearrange("p j (c i) -> p c j i", i=LINE))
 
-        def round_w3(mb):
-            dst = w3_bf[:, mb].rearrange("p (c i) j -> p c j i", i=2)
-            src = w3_raw[:].rearrange("p j (c i mb) -> p mb c j i", i=2, mb=2)[:, mb]
-            nc.scalar.copy(dst, src)
+        def round_w3(engine_copy, n0, n1):
+            dst = w3_bf[:, n0:n1, :].rearrange("p (c i) j -> p c j i", i=LINE)
+            engine_copy(dst, w3_raw[:, :, n0:n1].rearrange("p j (c i) -> p c j i", i=LINE))
 
         def quantise_wo(b, rounded, n0, n1):
             nc.vector.quantize_mx(
                 out=wo_codes[b][:, n0:n1].bitcast(FP8X4),
                 scales=wo_scales[b][:, n0:n1],
-                in_=rounded[:].rearrange("p mb m j -> p (mb m j)")[:, PACK * n0 : PACK * n1],
+                in_=rounded[:].rearrange("p n j -> p (n j)")[:, PACK * n0 : PACK * n1],
             )
 
         def warm_up():
@@ -243,7 +241,7 @@ def tile_picked_haar_gelu_p_kernel(tc, x_words, x_scales, w1, w2, w3, offs, out)
                 for t in reversed(range(PACK)):
                     product_second_half(z, d, t, z == PASSES - 1 and t == PACK - 1, z == 0 and t == 0)
 
-        round_w2(nc.scalar.copy, 0)
+        round_w2(nc.scalar.copy, 0, 0, N)
         gelu_first_half(0, 0, HALF)
         for v0, v1 in FIRST_PIECES:
             gelu_first_half(1, v0, v1)
@@ -251,10 +249,10 @@ def tile_picked_haar_gelu_p_kernel(tc, x_words, x_scales, w1, w2, w3, offs, out)
         for v0, v1 in SECOND_PIECES:
             gelu_second_half(1, v0, v1)
 
-        round_w2(nc.vector.tensor_copy, 1)
-        w3_bf = tile_after([P, 2, P, PACK], BF16, "w3_bf", "w1_codes00")
+        round_w2(nc.vector.tensor_copy, 1, 0, N)
+        w3_bf = tile_after([P, N, PACK], BF16, "w3_bf", "w1_codes00")
         for mb in range(2):
-            round_w3(mb)
+            round_w3(nc.scalar.copy, mb * P, (mb + 1) * P)
         quantise_wo(0, w2_bf, 0, N)
 
         band_bf = [tile([P, 2, HALF, PACK], BF16, "band_bf%d" % s) for s in range(2)]
@@ -281,4 +279,4 @@ def tile_picked_haar_gelu_p_kernel(tc, x_words, x_scales, w1, w2, w3, offs, out)
             halve_on_scalar(s, 0)
         halve_on_vector(0, 1)
         halve_on_scalar(1, 1)
-        nc.sync.dma_start(out=out.rearrange("(p mb) v -> p (mb v)", mb=2), in_=result[:].rearrange("p mb s v -> p (mb s v)"))
+        nc.sync.dma_start(out=out.rearrange("(mb p) v -> p mb v", mb=2), in_=result[:].rearrange("p mb s v -> p mb (s v)"))

@@ -65,11 +65,7 @@ def tile_picked_haar_gelu_p_kernel(tc, x_words, x_scales, w1, w2, w3, offs, out)
         preload_out = tile([P, 8], F32, "preload_out")
         pre_first = [ps.tile([P, PACK, HALF], F32, name="pre_first%d" % u) for u in range(2)]
         pre_second = [ps.tile([P, PACK, HALF], F32, name="pre_second%d" % d) for d in range(2)]
-        warm_bank = ps.tile([P, S], F32, name="warm_bank")
-        acc = [[ps.tile([P, HALF], F32, name="acc0%d" % mb) for mb in range(2)], [ps.tile([P, HALF], F32, name="acc10")]]
-        warm_bf = tile([P, H], BF16, "warm_bf")
-        warm_codes = tile([P, P], U32, "warm_codes")
-        warm_scales = tile([P, P], U8, "warm_scales")
+        acc = [[ps.tile([P, HALF], F32, name="acc%d%d" % (s, mb)) for mb in range(2)] for s in range(2)]
         preload_in = tile([P, 8], F32, "preload_in")
 
         def load_words(z):
@@ -103,17 +99,6 @@ def tile_picked_haar_gelu_p_kernel(tc, x_words, x_scales, w1, w2, w3, offs, out)
                 out=wo_codes[b][:, n0:n1].bitcast(FP8X4),
                 scales=wo_scales[b][:, n0:n1],
                 in_=rounded[:].rearrange("p n j -> p (n j)")[:, PACK * n0 : PACK * n1],
-            )
-
-        def warm_up():
-            nc.tensor.matmul_mx(
-                out=warm_bank[:],
-                lhsT=warm_codes[:].bitcast(FP8X4),
-                lhsT_scale=warm_scales[:],
-                rhs=picked_words[0][:].bitcast(FP4X4),
-                rhs_scale=picked_scales[0][:],
-                start=True,
-                stop=True,
             )
 
         def first_product(bank_range, z, s, d, t, start, stop):
@@ -210,11 +195,6 @@ def tile_picked_haar_gelu_p_kernel(tc, x_words, x_scales, w1, w2, w3, offs, out)
         load_rows(w2_raw[1][:], w2, 2, PACK)
         w3_raw = tile_after([P, PACK, N], F32, "w3_raw", "pass0_raw")
         load_rows(w3_raw[:], w3, 0, PACK)
-
-        nc.scalar.copy(warm_bf[:], pass0_raw[:, 0, :])
-        nc.vector.quantize_mx(out=warm_codes[:].bitcast(FP8X4), scales=warm_scales[:], in_=warm_bf[:])
-        warm_up()
-        acc[1].append(ps.tile([P, HALF], F32, name="acc11", tag="warm_bank"))
 
         round_w1(nc.scalar.copy, pass0_raw, 0, 0, PACK, 0, 0, P)
         round_w1(nc.vector.tensor_copy, pass0_raw, 0, 0, PACK, 1, 0, VECTOR_SHARE_PASS0)

@@ -27,7 +27,7 @@ QUADRANT_ROWS = 4
 SHIFT = 16
 LINE = 4
 VECTOR_SHARE_PASS0 = 88
-VECTOR_SHARE_LAST = 40
+VECTOR_SHARE_PASS1 = (84, 64)
 FIRST_PIECES = ((0, 32), (32, 64), (64, HALF))
 SECOND_PIECES = ((0, 96), (96, HALF))
 
@@ -50,7 +50,7 @@ def tile_picked_haar_gelu_p_kernel(tc, x_words, x_scales, w1, w2, w3, offs, out)
         word_table = [tile([P, T], U16, "word_table%d" % z) for z in range(PASSES)]
         picked_words = [tile([P, S], U16, "picked_words%d" % z) for z in range(PASSES)]
         pass0_raw = tile([P, PACK, H], F32, "pass0_raw")
-        pass1_raw = [tile([P, 2, H], F32, "pass1_raw%d" % h) for h in range(2)]
+        pass1_raw = tile([P, PACK, H], F32, "pass1_raw")
         w1_bf = [[tile([P, 2, P, PACK], BF16, "w1_bf%d%d" % (z, u)) for u in range(2)] for z in range(PASSES)]
         w1_codes = [[tile([P, 2 * P], U32, "w1_codes%d%d" % (z, u)) for u in range(2)] for z in range(PASSES)]
         w1_scales = [[tile([P, 2 * P], U8, "w1_scales%d%d" % (z, u)) for u in range(2)] for z in range(PASSES)]
@@ -61,7 +61,7 @@ def tile_picked_haar_gelu_p_kernel(tc, x_words, x_scales, w1, w2, w3, offs, out)
         hidden_second = [tile([P, HALF, PACK], F32, "hidden_second%d" % d) for d in range(2)]
         band_codes = [[tile([P, HALF], U32, "band_codes%d%d" % (s, b)) for b in range(2)] for s in range(2)]
         band_scales = [[tile([P, HALF], U8, "band_scales%d%d" % (s, b)) for b in range(2)] for s in range(2)]
-        result = tile([P, 2, 2, HALF], F32, "result")
+        result = [tile([P, 2, HALF], F32, "result%d" % mb) for mb in range(2)]
         preload_out = tile([P, 8], F32, "preload_out")
         pre_first = [ps.tile([P, PACK, HALF], F32, name="pre_first%d" % u) for u in range(2)]
         pre_second = [ps.tile([P, PACK, HALF], F32, name="pre_second%d" % d) for d in range(2)]
@@ -86,9 +86,9 @@ def tile_picked_haar_gelu_p_kernel(tc, x_words, x_scales, w1, w2, w3, offs, out)
                 in_=w1_bf[z][u][:].rearrange("p t m j -> p (t m j)")[:, PACK * c0 : PACK * c1],
             )
 
-        def round_w2(engine_copy, h, n0, n1):
-            dst = w2_bf[:, n0:n1, 2 * h : 2 * h + 2].rearrange("p (c i) j -> p c j i", i=LINE)
-            engine_copy(dst, w2_raw[h][:, :, n0:n1].rearrange("p j (c i) -> p c j i", i=LINE))
+        def round_w2(engine_copy, mb):
+            dst = w2_bf[:, mb * P : (mb + 1) * P, :].rearrange("p (c i) j -> p c j i", i=LINE)
+            engine_copy(dst, w2_raw[mb][:].rearrange("p j (c i) -> p c j i", i=LINE))
 
         def round_w3(engine_copy, n0, n1):
             dst = w3_bf[:, n0:n1, :].rearrange("p (c i) j -> p c j i", i=LINE)
@@ -164,10 +164,10 @@ def tile_picked_haar_gelu_p_kernel(tc, x_words, x_scales, w1, w2, w3, offs, out)
             )
 
         def halve_on_scalar(s, mb):
-            nc.scalar.activation(out=result[:, mb, s, :], in_=acc[s][mb][:], func=COPY, scale=0.5)
+            nc.scalar.activation(out=result[mb][:, s, :], in_=acc[s][mb][:], func=COPY, scale=0.5)
 
         def halve_on_vector(s, mb):
-            nc.vector.tensor_scalar(out=result[:, mb, s, :], in0=acc[s][mb][:], scalar1=0.5, scalar2=None, op0=MULT)
+            nc.vector.tensor_scalar(out=result[mb][:, s, :], in0=acc[s][mb][:], scalar1=0.5, scalar2=None, op0=MULT)
 
         nc.gpsimd.memset(scale_table[:].bitcast(I32), 0)
         nc.vector.memset(preload_in[:], 0.0)
@@ -182,17 +182,16 @@ def tile_picked_haar_gelu_p_kernel(tc, x_words, x_scales, w1, w2, w3, offs, out)
         nc.scalar.activation(out=preload_out[:], in_=preload_in[:], func=GELU)
         for h in range(2):
             load_rows(pass0_raw[:, 2 * h : 2 * h + 2, :], w1[: P * PACK, :], 2 * h, 2 * h + 2)
-        for h in range(2):
-            load_rows(pass1_raw[h][:], w1[P * PACK :, :], 2 * h, 2 * h + 2)
-        w2_raw = [tile([P, 2, N], F32, "w2_raw0")]
-        load_rows(w2_raw[0][:], w2, 0, 2)
+        load_rows(pass1_raw[:], w1[P * PACK :, :], 0, PACK)
+        w2_raw = [tile([P, PACK, P], F32, "w2_raw0")]
+        load_rows(w2_raw[0][:], w2[:, :P], 0, PACK)
 
         for z in range(PASSES):
             nc.vector.tensor_copy(picked_words[z][:], word_table[z][:].indirect(offsets[:]))
         nc.vector.tensor_copy(picked_scales[0][:], scale_table[:].indirect(offsets[:]))
         nc.sync.dma_start(out=picked_scales[1][0 : P - SHIFT, :].bitcast(I32), in_=picked_scales[0][SHIFT:P, :].bitcast(I32))
-        w2_raw.append(tile_after([P, 2, N], F32, "w2_raw1", "scale_table"))
-        load_rows(w2_raw[1][:], w2, 2, PACK)
+        w2_raw.append(tile_after([P, PACK, P], F32, "w2_raw1", "scale_table"))
+        load_rows(w2_raw[1][:], w2[:, P:], 0, PACK)
         w3_raw = tile_after([P, PACK, N], F32, "w3_raw", "pass0_raw")
         load_rows(w3_raw[:], w3, 0, PACK)
 
@@ -205,11 +204,9 @@ def tile_picked_haar_gelu_p_kernel(tc, x_words, x_scales, w1, w2, w3, offs, out)
             for d in range(2):
                 product_first_half(0, d, t, t % 2 == 0 and d == 0, False)
 
-        round_w1(nc.vector.tensor_copy, pass1_raw[0], 1, 0, 2, 0, 0, P)
-        round_w1(nc.scalar.copy, pass1_raw[0], 1, 0, 2, 1, 0, P)
-        round_w1(nc.vector.tensor_copy, pass1_raw[1], 1, 2, PACK, 0, 0, P, 2)
-        round_w1(nc.scalar.copy, pass1_raw[1], 1, 2, PACK, 1, VECTOR_SHARE_LAST, P, 2)
-        round_w1(nc.vector.tensor_copy, pass1_raw[1], 1, 2, PACK, 1, 0, VECTOR_SHARE_LAST, 2)
+        for u in range(2):
+            round_w1(nc.vector.tensor_copy, pass1_raw, 1, 0, PACK, u, 0, VECTOR_SHARE_PASS1[u])
+            round_w1(nc.scalar.copy, pass1_raw, 1, 0, PACK, u, VECTOR_SHARE_PASS1[u], P)
         for i in range(2):
             quantise_w1(1, 0, i * P, (i + 1) * P)
         quantise_w1(1, 1, 0, 2 * P)
@@ -221,7 +218,7 @@ def tile_picked_haar_gelu_p_kernel(tc, x_words, x_scales, w1, w2, w3, offs, out)
                 for t in reversed(range(PACK)):
                     product_second_half(z, d, t, z == PASSES - 1 and t == PACK - 1, z == 0 and t == 0)
 
-        round_w2(nc.scalar.copy, 0, 0, N)
+        round_w2(nc.scalar.copy, 0)
         gelu_first_half(0, 0, HALF)
         for v0, v1 in FIRST_PIECES:
             gelu_first_half(1, v0, v1)
@@ -229,7 +226,7 @@ def tile_picked_haar_gelu_p_kernel(tc, x_words, x_scales, w1, w2, w3, offs, out)
         for v0, v1 in SECOND_PIECES:
             gelu_second_half(1, v0, v1)
 
-        round_w2(nc.vector.tensor_copy, 1, 0, N)
+        round_w2(nc.vector.tensor_copy, 1)
         w3_bf = tile_after([P, N, PACK], BF16, "w3_bf", "w1_codes00")
         for mb in range(2):
             round_w3(nc.scalar.copy, mb * P, (mb + 1) * P)
@@ -259,4 +256,5 @@ def tile_picked_haar_gelu_p_kernel(tc, x_words, x_scales, w1, w2, w3, offs, out)
             halve_on_scalar(s, 0)
         halve_on_vector(0, 1)
         halve_on_scalar(1, 1)
-        nc.sync.dma_start(out=out.rearrange("(mb p) v -> p mb v", mb=2), in_=result[:].rearrange("p mb s v -> p mb (s v)"))
+        for mb in range(2):
+            nc.sync.dma_start(out=out[mb * P : (mb + 1) * P, :], in_=result[mb][:].rearrange("p s v -> p (s v)"))

@@ -27,9 +27,9 @@ QUADRANT_ROWS = 4
 SHIFT = 16
 LINE = 4
 VECTOR_SHARE_PASS0 = 88
-VECTOR_SHARE_PASS1 = (84, 64)
-FIRST_PIECES = ((0, 32), (32, 64), (64, HALF))
-SECOND_PIECES = ((0, 96), (96, HALF))
+VECTOR_SHARE_PASS1 = (88, 72)
+FIRST_PIECES = ((0, 48), (48, HALF))
+SECOND_PIECES = ((0, 48), (48, HALF))
 
 
 def tile_picked_haar_gelu_p_kernel(tc, x_words, x_scales, w1, w2, w3, offs, out):
@@ -63,9 +63,8 @@ def tile_picked_haar_gelu_p_kernel(tc, x_words, x_scales, w1, w2, w3, offs, out)
         band_scales = [[tile([P, HALF], U8, "band_scales%d%d" % (s, b)) for b in range(2)] for s in range(2)]
         result = [tile([P, 2, HALF], F32, "result%d" % mb) for mb in range(2)]
         preload_out = tile([P, 8], F32, "preload_out")
-        pre_first = [ps.tile([P, PACK, HALF], F32, name="pre_first%d" % u) for u in range(2)]
+        pre_first = [[ps.tile([P, 2, HALF], F32, name="pre_first%d%d" % (u, d)) for d in range(2)] for u in range(2)]
         pre_second = [ps.tile([P, PACK, HALF], F32, name="pre_second%d" % d) for d in range(2)]
-        acc = [[ps.tile([P, HALF], F32, name="acc%d%d" % (s, mb)) for mb in range(2)] for s in range(2)]
         preload_in = tile([P, 8], F32, "preload_in")
 
         def load_words(z):
@@ -115,14 +114,14 @@ def tile_picked_haar_gelu_p_kernel(tc, x_words, x_scales, w1, w2, w3, offs, out)
             )
 
         def product_first_half(z, d, t, start, stop):
-            first_product(pre_first[t // 2][:, 2 * d + t % 2, :], z, 0, d, t, start, stop)
+            first_product(pre_first[t // 2][d][:, t % 2, :], z, 0, d, t, start, stop)
 
         def product_second_half(z, d, t, start, stop):
             first_product(pre_second[d][:, t, :], z, 1, d, t, start, stop)
 
-        def gelu_first_half(u, v0, v1):
-            src = pre_first[u][:, :, v0:v1].rearrange("p (d t) v -> p d v t", d=2)
-            nc.scalar.activation(out=hidden_first[:, u, :, v0:v1, :], in_=src, func=GELU)
+        def gelu_first_half(u, d, v0, v1):
+            src = pre_first[u][d][:, :, v0:v1].rearrange("p t v -> p v t")
+            nc.scalar.activation(out=hidden_first[:, u, d, v0:v1, :], in_=src, func=GELU)
 
         def gelu_second_half(d, v0, v1):
             src = pre_second[d][:, :, v0:v1].rearrange("p t v -> p v t")
@@ -198,39 +197,46 @@ def tile_picked_haar_gelu_p_kernel(tc, x_words, x_scales, w1, w2, w3, offs, out)
         round_w1(nc.scalar.copy, pass0_raw, 0, 0, PACK, 0, 0, P)
         round_w1(nc.vector.tensor_copy, pass0_raw, 0, 0, PACK, 1, 0, VECTOR_SHARE_PASS0)
         round_w1(nc.scalar.copy, pass0_raw, 0, 0, PACK, 1, VECTOR_SHARE_PASS0, P)
-        for u in range(2):
-            quantise_w1(0, u, 0, 2 * P)
+        for i in range(2):
+            quantise_w1(0, 0, i * P, (i + 1) * P)
+        quantise_w1(0, 1, 0, 2 * P)
         for t in range(PACK):
             for d in range(2):
-                product_first_half(0, d, t, t % 2 == 0 and d == 0, False)
+                product_first_half(0, d, t, t % 2 == 0, False)
+        for t in range(PACK):
+            product_second_half(0, 0, t, t == 0, False)
 
         for u in range(2):
             round_w1(nc.vector.tensor_copy, pass1_raw, 1, 0, PACK, u, 0, VECTOR_SHARE_PASS1[u])
             round_w1(nc.scalar.copy, pass1_raw, 1, 0, PACK, u, VECTOR_SHARE_PASS1[u], P)
-        for i in range(2):
-            quantise_w1(1, 0, i * P, (i + 1) * P)
-        quantise_w1(1, 1, 0, 2 * P)
         for t in range(PACK):
+            quantise_w1(1, t // 2, (t % 2) * P, (t % 2 + 1) * P)
+        for u in range(2):
             for d in range(2):
-                product_first_half(1, d, t, False, t % 2 == 1 and d == 1)
-        for d in range(2):
-            for z in reversed(range(PASSES)):
-                for t in reversed(range(PACK)):
-                    product_second_half(z, d, t, z == PASSES - 1 and t == PACK - 1, z == 0 and t == 0)
+                for t in (2 * u, 2 * u + 1):
+                    product_first_half(1, d, t, False, t % 2 == 1)
+        for t in reversed(range(PACK)):
+            product_second_half(1, 0, t, False, t == 0)
+        for z in reversed(range(PASSES)):
+            for t in reversed(range(PACK)):
+                product_second_half(z, 1, t, z == PASSES - 1 and t == PACK - 1, z == 0 and t == 0)
 
         round_w2(nc.scalar.copy, 0)
-        gelu_first_half(0, 0, HALF)
+        for d in range(2):
+            gelu_first_half(0, d, 0, HALF)
         for v0, v1 in FIRST_PIECES:
-            gelu_first_half(1, v0, v1)
+            for d in range(2):
+                gelu_first_half(1, d, v0, v1)
         gelu_second_half(0, 0, HALF)
         for v0, v1 in SECOND_PIECES:
             gelu_second_half(1, v0, v1)
 
+        quantise_wo(0, w2_bf, 0, P)
         round_w2(nc.vector.tensor_copy, 1)
         w3_bf = tile_after([P, N, PACK], BF16, "w3_bf", "w1_codes00")
         for mb in range(2):
             round_w3(nc.scalar.copy, mb * P, (mb + 1) * P)
-        quantise_wo(0, w2_bf, 0, N)
+        quantise_wo(0, w2_bf, P, N)
 
         band_bf = [tile([P, 2, HALF, PACK], BF16, "band_bf%d" % s) for s in range(2)]
         for v0, v1 in FIRST_PIECES:
@@ -246,6 +252,10 @@ def tile_picked_haar_gelu_p_kernel(tc, x_words, x_scales, w1, w2, w3, offs, out)
             quantise_band(1, b)
         quantise_wo(1, w3_bf, P, N)
 
+        acc = [
+            [ps.tile([P, HALF], F32, name="acc%d%d" % (s, mb), tag="pre_first%d%d" % (s, mb)) for mb in range(2)]
+            for s in range(2)
+        ]
         for s in range(2):
             for mb in range(2):
                 second_product(s, 0, mb)

from contextlib import ExitStack

import concourse.mybir as mybir

K, T, S, V, H, N = 1024, 1024, 512, 256, 512, 256
FLOPS = 2 * K * H * S + 2 * 2 * H * N * V

F32 = mybir.dt.float32
BF16 = mybir.dt.bfloat16
I32 = mybir.dt.int32
U32 = mybir.dt.uint32
U16 = mybir.dt.uint16
U8 = mybir.dt.uint8
FP8X4 = mybir.dt.float8_e4m3fn_x4
FP4X4 = mybir.dt.float4_e2m1fn_x4
GELU = mybir.ActivationFunctionType.Gelu_apprx_tanh
COPY = mybir.ActivationFunctionType.Copy
ADD = mybir.AluOpType.add
SUB = mybir.AluOpType.subtract
MULT = mybir.AluOpType.mult

P = 128
PACK = 4
PASSES = K // (P * PACK)
HALF = V // 2
QUADRANT_ROWS = 4
SHIFT = 16
LINE = 4
VECTOR_SHARE_PASS0 = 88
VECTOR_SHARE_PASS1 = (88, 72)
FIRST_PIECES = ((0, 48), (48, HALF))
SECOND_PIECES = ((0, 48), (48, HALF))


def tile_picked_haar_gelu_p_kernel(tc, x_words, x_scales, w1, w2, w3, offs, out):
    nc = tc.nc
    with ExitStack() as ctx:
        sb = ctx.enter_context(tc.tile_pool(name="sb", bufs=1))
        ps = ctx.enter_context(tc.psum_pool(name="ps", bufs=1))

        def tile(shape, dtype, name):
            return sb.tile(shape, dtype, name=name, align_bytes=64)

        def tile_after(shape, dtype, name, earlier):
            return sb.tile(shape, dtype, name=name, tag=earlier, align_bytes=64)

        offsets = tile([P, S // 16], U16, "offsets")
        scale_table = tile([P, T], U8, "scale_table")
        picked_scales = [tile([P, S], U8, "picked_scales"), tile([P, S], U8, "moved_scales")]
        word_table = [tile([P, T], U16, "word_table%d" % z) for z in range(PASSES)]
        picked_words = [tile([P, S], U16, "picked_words%d" % z) for z in range(PASSES)]
        pass0_raw = tile([P, PACK, H], F32, "pass0_raw")
        pass1_raw = tile([P, PACK, H], F32, "pass1_raw")
        w1_bf = [[tile([P, 2, P, PACK], BF16, "w1_bf%d%d" % (z, u)) for u in range(2)] for z in range(PASSES)]
        w1_codes = [[tile([P, 2 * P], U32, "w1_codes%d%d" % (z, u)) for u in range(2)] for z in range(PASSES)]
        w1_scales = [[tile([P, 2 * P], U8, "w1_scales%d%d" % (z, u)) for u in range(2)] for z in range(PASSES)]
        w2_bf = tile([P, N, PACK], BF16, "w2_bf")
        wo_codes = [tile([P, N], U32, "wo_codes%d" % b) for b in range(2)]
        wo_scales = [tile([P, N], U8, "wo_scales%d" % b) for b in range(2)]
        hidden_first = tile([P, 2, 2, HALF, 2], F32, "hidden_first")
        hidden_second = [tile([P, HALF, PACK], F32, "hidden_second%d" % d) for d in range(2)]
        band_codes = [[tile([P, HALF], U32, "band_codes%d%d" % (s, b)) for b in range(2)] for s in range(2)]
        band_scales = [[tile([P, HALF], U8, "band_scales%d%d" % (s, b)) for b in range(2)] for s in range(2)]
        result = [tile([P, 2, HALF], F32, "result%d" % mb) for mb in range(2)]
        preload_out = tile([P, 8], F32, "preload_out")
        pre_first = [[ps.tile([P, 2, HALF], F32, name="pre_first%d%d" % (u, d)) for d in range(2)] for u in range(2)]
        pre_second = [ps.tile([P, PACK, HALF], F32, name="pre_second%d" % d) for d in range(2)]
        preload_in = tile([P, 8], F32, "preload_in")

        def load_words(z):
            nc.sync.dma_start(out=word_table[z][:].bitcast(I32), in_=x_words[z].bitcast(I32))

        def load_rows(raw, rows, j0, j1):
            nc.sync.dma_start(out=raw, in_=rows.rearrange("(p j) n -> p j n", j=PACK)[:, j0:j1, :])

        def round_w1(engine_copy, raw, z, j0, j1, u, m0, m1, first_j=0):
            dst = w1_bf[z][u][:, :, m0:m1, j0:j1].rearrange("p t m j -> p m j t")
            src = raw[:, j0 - first_j : j1 - first_j, PACK * m0 : PACK * m1].rearrange("p j (m t) -> p m j t", t=PACK)
            engine_copy(dst, src[:, :, :, 2 * u : 2 * u + 2])

        def quantise_w1(z, u, c0, c1):
            nc.vector.quantize_mx(
                out=w1_codes[z][u][:, c0:c1].bitcast(FP8X4),
                scales=w1_scales[z][u][:, c0:c1],
                in_=w1_bf[z][u][:].rearrange("p t m j -> p (t m j)")[:, PACK * c0 : PACK * c1],
            )

        def round_w2(engine_copy, mb):
            dst = w2_bf[:, mb * P : (mb + 1) * P, :].rearrange("p (c i) j -> p c j i", i=LINE)
            engine_copy(dst, w2_raw[mb][:].rearrange("p j (c i) -> p c j i", i=LINE))

        def round_w3(engine_copy, n0, n1):
            dst = w3_bf[:, n0:n1, :].rearrange("p (c i) j -> p c j i", i=LINE)
            engine_copy(dst, w3_raw[:, :, n0:n1].rearrange("p j (c i) -> p c j i", i=LINE))

        def quantise_wo(b, rounded, n0, n1):
            nc.vector.quantize_mx(
                out=wo_codes[b][:, n0:n1].bitcast(FP8X4),
                scales=wo_scales[b][:, n0:n1],
                in_=rounded[:].rearrange("p n j -> p (n j)")[:, PACK * n0 : PACK * n1],
            )

        def first_product(bank_range, z, s, d, t, start, stop):
            cols = slice((t % 2) * P, (t % 2 + 1) * P)
            entries = slice(d * V + s * HALF, d * V + (s + 1) * HALF)
            nc.tensor.matmul_mx(
                out=bank_range,
                lhsT=w1_codes[z][t // 2][:, cols].bitcast(FP8X4),
                lhsT_scale=w1_scales[z][t // 2][:, cols],
                rhs=picked_words[z][:, entries].bitcast(FP4X4),
                rhs_scale=picked_scales[z][:, entries],
                start=start,
                stop=stop,
            )

        def product_first_half(z, d, t, start, stop):
            first_product(pre_first[t // 2][d][:, t % 2, :], z, 0, d, t, start, stop)

        def product_second_half(z, d, t, start, stop):
            first_product(pre_second[d][:, t, :], z, 1, d, t, start, stop)

        def gelu_first_half(u, d, v0, v1):
            src = pre_first[u][d][:, :, v0:v1].rearrange("p t v -> p v t")
            nc.scalar.activation(out=hidden_first[:, u, d, v0:v1, :], in_=src, func=GELU)

        def gelu_second_half(d, v0, v1):
            src = pre_second[d][:, :, v0:v1].rearrange("p t v -> p v t")
            nc.scalar.activation(out=hidden_second[d][:, v0:v1, :], in_=src, func=GELU)

        def band_first_half(b, v0, v1):
            nc.vector.tensor_tensor(
                out=band_bf[0][:, b, v0:v1, :].rearrange("p v (u t) -> p v u t", u=2),
                in0=hidden_first[:, :, 0, v0:v1, :].rearrange("p u v t -> p v u t"),
                in1=hidden_first[:, :, 1, v0:v1, :].rearrange("p u v t -> p v u t"),
                op=(ADD if b == 0 else SUB),
            )

        def band_second_half(b, v0, v1):
            nc.vector.tensor_tensor(
                out=band_bf[1][:, b, v0:v1, :],
                in0=hidden_second[0][:, v0:v1, :],
                in1=hidden_second[1][:, v0:v1, :],
                op=(ADD if b == 0 else SUB),
            )

        def quantise_band(s, b):
            nc.vector.quantize_mx(
                out=band_codes[s][b][:].bitcast(FP8X4),
                scales=band_scales[s][b][:],
                in_=band_bf[s][:, b, :, :].rearrange("p v t -> p (v t)"),
            )

        def second_product(s, b, mb):
            cols = slice(mb * P, (mb + 1) * P)
            nc.tensor.matmul_mx(
                out=acc[s][mb][:],
                lhsT=wo_codes[b][:, cols].bitcast(FP8X4),
                lhsT_scale=wo_scales[b][:, cols],
                rhs=band_codes[s][b][:].bitcast(FP8X4),
                rhs_scale=band_scales[s][b][:],
                start=(b == 0),
                stop=(b == 1),
            )

        def halve_on_scalar(s, mb):
            nc.scalar.activation(out=result[mb][:, s, :], in_=acc[s][mb][:], func=COPY, scale=0.5)

        def halve_on_vector(s, mb):
            nc.vector.tensor_scalar(out=result[mb][:, s, :], in0=acc[s][mb][:], scalar1=0.5, scalar2=None, op0=MULT)

        nc.gpsimd.memset(scale_table[:].bitcast(I32), 0)
        nc.vector.memset(preload_in[:], 0.0)
        nc.vector.memset(picked_scales[1][:].bitcast(I32), 0)

        load_words(0)
        nc.sync.dma_start(out=offsets[:], in_=offs)
        load_words(1)
        scale_rows = x_scales.rearrange("z (q r) n -> r q z n", r=QUADRANT_ROWS)
        for r in range(QUADRANT_ROWS):
            nc.sync.dma_start(out=scale_table[r:P:SHIFT, :].bitcast(I32), in_=scale_rows[r].bitcast(I32))
        nc.scalar.activation(out=preload_out[:], in_=preload_in[:], func=GELU)
        for h in range(2):
            load_rows(pass0_raw[:, 2 * h : 2 * h + 2, :], w1[: P * PACK, :], 2 * h, 2 * h + 2)
        load_rows(pass1_raw[:], w1[P * PACK :, :], 0, PACK)
        w2_raw = [tile([P, PACK, P], F32, "w2_raw0")]
        load_rows(w2_raw[0][:], w2[:, :P], 0, PACK)

        for z in range(PASSES):
            nc.vector.tensor_copy(picked_words[z][:], word_table[z][:].indirect(offsets[:]))
        nc.vector.tensor_copy(picked_scales[0][:], scale_table[:].indirect(offsets[:]))
        nc.sync.dma_start(out=picked_scales[1][0 : P - SHIFT, :].bitcast(I32), in_=picked_scales[0][SHIFT:P, :].bitcast(I32))
        w2_raw.append(tile_after([P, PACK, P], F32, "w2_raw1", "scale_table"))
        load_rows(w2_raw[1][:], w2[:, P:], 0, PACK)
        w3_raw = tile_after([P, PACK, N], F32, "w3_raw", "pass0_raw")
        load_rows(w3_raw[:], w3, 0, PACK)

        round_w1(nc.scalar.copy, pass0_raw, 0, 0, PACK, 0, 0, P)
        round_w1(nc.vector.tensor_copy, pass0_raw, 0, 0, PACK, 1, 0, VECTOR_SHARE_PASS0)
        round_w1(nc.scalar.copy, pass0_raw, 0, 0, PACK, 1, VECTOR_SHARE_PASS0, P)
        for i in range(2):
            quantise_w1(0, 0, i * P, (i + 1) * P)
        quantise_w1(0, 1, 0, 2 * P)
        for t in range(PACK):
            for d in range(2):
                product_first_half(0, d, t, t % 2 == 0, False)
        for t in range(PACK):
            product_second_half(0, 0, t, t == 0, False)

        for u in range(2):
            round_w1(nc.vector.tensor_copy, pass1_raw, 1, 0, PACK, u, 0, VECTOR_SHARE_PASS1[u])
            round_w1(nc.scalar.copy, pass1_raw, 1, 0, PACK, u, VECTOR_SHARE_PASS1[u], P)
        for t in range(PACK):
            quantise_w1(1, t // 2, (t % 2) * P, (t % 2 + 1) * P)
        for u in range(2):
            for d in range(2):
                for t in (2 * u, 2 * u + 1):
                    product_first_half(1, d, t, False, t % 2 == 1)
        for t in reversed(range(PACK)):
            product_second_half(1, 0, t, False, t == 0)
        for z in reversed(range(PASSES)):
            for t in reversed(range(PACK)):
                product_second_half(z, 1, t, z == PASSES - 1 and t == PACK - 1, z == 0 and t == 0)

        round_w2(nc.scalar.copy, 0)
        for d in range(2):
            gelu_first_half(0, d, 0, HALF)
        for v0, v1 in FIRST_PIECES:
            for d in range(2):
                gelu_first_half(1, d, v0, v1)
        gelu_second_half(0, 0, HALF)
        for v0, v1 in SECOND_PIECES:
            gelu_second_half(1, v0, v1)

        quantise_wo(0, w2_bf, 0, P)
        round_w2(nc.vector.tensor_copy, 1)
        w3_bf = tile_after([P, N, PACK], BF16, "w3_bf", "w1_codes00")
        for mb in range(2):
            round_w3(nc.scalar.copy, mb * P, (mb + 1) * P)
        quantise_wo(0, w2_bf, P, N)

        band_bf = [tile([P, 2, HALF, PACK], BF16, "band_bf%d" % s) for s in range(2)]
        for v0, v1 in FIRST_PIECES:
            for b in range(2):
                band_first_half(b, v0, v1)
        for b in range(2):
            quantise_band(0, b)
        for v0, v1 in SECOND_PIECES:
            for b in range(2):
                band_second_half(b, v0, v1)
        quantise_wo(1, w3_bf, 0, P)
        for b in range(2):
            quantise_band(1, b)
        quantise_wo(1, w3_bf, P, N)

        acc = [
            [ps.tile([P, HALF], F32, name="acc%d%d" % (s, mb), tag="pre_first%d%d" % (s, mb)) for mb in range(2)]
            for s in range(2)
        ]
        for s in range(2):
            for mb in range(2):
                second_product(s, 0, mb)
        for mb in range(2):
            for s in range(2):
                second_product(s, 1, mb)
        for s in range(2):
            halve_on_scalar(s, 0)
        halve_on_vector(0, 1)
        halve_on_scalar(1, 1)
        for mb in range(2):
            nc.sync.dma_start(out=out[mb * P : (mb + 1) * P, :], in_=result[mb][:].rearrange("p s v -> p (s v)"))
